import numpy as np, ml_dtypes
CORES = [9,25,41,57]
N = 4
import mx_ref
BF = ml_dtypes.bfloat16
def gcols(t, e):
    v = np.concatenate([t.reshape(8, 16, -1, 4), np.zeros((8, 16, 1, 4), BF)], axis=2)
    return np.ascontiguousarray(np.stack([v[g][:, e[g]] for g in range(8)])).reshape(128, -1)
def tile(rs):
    return np.stack(rs, axis=2).reshape(128, -1).astype(BF)
def cut(t, i, w=512):
    return t[:, w * i:w * i + w]
def pick(q, e):
    c = np.concatenate([q[0].reshape(128, -1, 4), np.zeros((128, 1, 4), np.uint8)], axis=1); s = np.concatenate([q[1], np.ones((16, 1), np.uint8)], axis=1)
    return (np.ascontiguousarray(c[:, e].reshape(128, -1)), np.ascontiguousarray(s[:, e]))
def join(*qs):
    return (np.concatenate([q[0] for q in qs], axis=1), np.concatenate([q[1] for q in qs], axis=1))
def put(q, e, v):
    c, s = q[0].reshape(128, -1, 4).copy(), q[1].copy(); c[:, e] = v[0].reshape(128, -1, 4); s[:, e] = v[1]
    return (c.reshape(128, -1), s)
def pk(c, s):
    return (np.ascontiguousarray(c), mx_ref.live(s))
def emit(q):
    return q[0], q[1]
def packed(v, rng):
    q = [mx_ref.quantize(np.ascontiguousarray(v[r])) for r in range(N)]
    return np.stack([a for a, b in q]), np.stack([mx_ref.plane(b, rng) for a, b in q])
def values_of_codes():
    e, c = np.zeros((128, 128, 4), np.float32), np.zeros((128, 2, 4), np.uint8)
    e[np.arange(128), np.arange(128), 0] = 1
    c[:127, :, 0] = np.arange(256).reshape(2, 128).T[:127]
    return mx_ref.matmul(mx_ref.quantize(e.reshape(128, 512).astype(BF)), (c.reshape(128, 8), np.full((16, 2), 127, np.uint8))).T.reshape(-1).astype(np.float64)
CODE_VALUE, SCALE_VALUE = values_of_codes(), 2.0 ** (np.arange(256) - 127.0)
def decode(q):
    return (CODE_VALUE[q[0]].reshape(16, 8, -1, 4) * SCALE_VALUE[q[1]][:, None, :, None] + 0.0).reshape(128, -1).astype(np.float32)
def f(rng, *shape):
    return mx_ref.flush((rng.standard_normal(shape, dtype=np.float32) * np.exp2(rng.integers(-2, 3, shape[:-1] + (1,)))).astype(BF))
def wide(rng, *shape, cols=0):
    v = rng.standard_normal(shape, dtype=np.float32) * np.exp2(rng.integers(-12, 13, shape)).astype(np.float32)
    if cols: v *= np.repeat(np.exp2(rng.integers(-cols, cols + 1, shape[:-2] + (1, shape[-1] // 4))) * (rng.random(shape[:-2] + (1, shape[-1] // 4)) > 0.0625), 4, axis=-1).astype(np.float32)
    return mx_ref.flush(v.astype(BF))
C = 384
def order(p):
    return np.argsort(-(p[::16] + np.float32(0.0)), axis=1, kind="stable")
def swap(qs, k, n):
    e = np.arange(1, n, 2)
    return [put(qs[r], e, pick(qs[r ^ k], e)) for r in range(N)]
def half(z):
    return mx_ref.quantize(np.ascontiguousarray((z * np.float32(0.5)).astype(BF).reshape(128, -1)))
def big(v, k):
    v = v.astype(np.float32) * np.float32(k)
    v[np.abs(v) < np.float32(2.0 ** -16)] = 0
    return v.astype(BF)
def numbers_of(rng):
    return {"x": big(f(rng, N, 128, 4 * C), 1), "ua": np.array(f(rng, N, 128, 512)), "ub": np.array(f(rng, N, 128, 512)), "v": np.array(f(rng, N, 128, 512))}
def weights(rng, w):
    c, p = packed(w, rng)
    return {"wc": c, "ws": p}
def still(rng):
    w = np.zeros((N, 128, 4, 128, 4), np.float32)
    i = np.arange(128)
    for b in range(4): w[:, i, b, i, b] = 32
    return weights(rng, w.reshape(N, 128, 2048).astype(BF))
def signs(rng):
    return np.stack([rng.permutation(8) % 2 * 2.0 - 1.0 for r in range(N)])
def setup_inputs(rng):
    return {**numbers_of(rng), **weights(rng, f(rng, N, 128, 2048))}
def setup_inputs_ties(rng):
    d = numbers_of(rng)
    e = rng.permutation(N)
    x = d["x"].reshape(N, 8, 16, C, 4)
    for r in range(N):
        k = np.zeros(C, int) if r == e[0] else rng.permutation(C) % 3
        a = x[r][:, :8, :3].copy()
        a[:, :, 2] = 0
        x[r][:, :8] = a[:, :, k]
    x[e[1]] = 0
    for n in ("ua", "ub"):
        u = d[n].reshape(N, 8, 16, 128, 4)
        u[:, :, 8:, ::16] = 0
        d[n] = u.reshape(N, 128, 512)
    w = np.array(f(rng, N, 128, 2048)).reshape(N, 8, 16, 4, 8, 16, 4)
    w[:, :, 8:, :, :, :8] = 0
    return {**d, "x": x.reshape(N, 128, 4 * C), **weights(rng, w.reshape(N, 128, 2048))}
def setup_inputs_near(rng):
    d = numbers_of(rng)
    x = np.zeros((N, 8, 16, C, 4), np.float32)
    m = np.arange(C) // 2
    x[:, :, 0, :, 0] = np.repeat(signs(rng)[::2], 2, axis=0)[:, :, None]
    for p, s in ((8, m), (10, (C // 2 - 1 - m) // 2)):
        g = ((s[:, None] >> np.arange(8)) & 1) * np.exp2(np.arange(8) - 23.0)
        x[:, :, p] = g[:, :4]
        x[:, :, p + 1] = g[:, 4:]
    x[:, :, 12:] = rng.integers(4, 8, (N, 8, 4, C, 4)) * rng.choice([-1.0, 1.0], (N, 8, 4, C, 4)) * 2.0 ** -20
    for n, p in (("ua", 8), ("ub", 10)):
        u = d[n].reshape(N, 128, 128, 4)
        u[:, :, ::16] = 0
        for h in range(0, 128, 16):
            u[:, h, h, 0] = 2.0 ** -28
            u[:, h + p:h + p + 2, h] = 2.0 ** -28
        d[n] = u.reshape(N, 128, 512)
    return {**d, "x": x.reshape(N, 128, 4 * C).astype(BF), **still(rng)}
def setup_inputs_huge(rng):
    d = numbers_of(rng)
    x = 2.0 ** 29 * (0.6 + 0.4 * rng.random((N, 128, C, 4)))
    both = np.repeat(rng.permutation(N // 2) < N // 4, 2)
    c = np.stack([rng.permutation(C) % 2 * 2.0 - 1.0 for r in range(N)])
    c[~both] = 1
    x *= c[:, None, :, None]
    g = signs(rng)
    g[both] = g[both][:, :1]
    for n, s in (("ua", g), ("ub", signs(rng))):
        u = d[n].reshape(N, 128, 128, 4)
        a = 2.0 ** 30 * (1 - 0.25 * rng.random((N, 128, 8, 4))) * s[:, None, :, None]
        u[:, :, ::16] = a.astype(np.float32).astype(BF)
        d[n] = u.reshape(N, 128, 512)
    return {**d, "x": x.astype(np.float32).reshape(N, 128, 4 * C).astype(BF), **still(rng)}
def setup_inputs_sizes(rng):
    d = setup_inputs(rng)
    k = np.concatenate([rng.permutation(4) for i in range(N // 4)]) * 5.0
    d["x"] = big(d["x"].astype(np.float32) * np.exp2(k).astype(np.float32)[:, None, None], 1)
    return d
def setup_inputs_spread(rng):
    d = setup_inputs(rng)
    d["x"] = big(wide(rng, N, 128, 4 * C, cols=6), 1)
    return d
def check_inputs(d):
    b = []
    for k in ("x", "ua", "ub", "v"):
        a = np.abs(d[k].astype(np.float32))
        if not (np.isfinite(a).all() and ((a == 0) | (a >= 2.0 ** -30) & (a <= 2.0 ** 30)).all()): b.append("a value of " + k)
    return b
def reference(x, ua, ub, v, wc, ws):
    lay = [pk(wc[r], ws[r]) for r in range(N)]
    now = [mx_ref.quantize(x[r]) for r in range(N)]
    orders, highs = [], []
    for l in range(2):
        s, n = (ua, ub)[l], C >> l
        d = decode(join(*now)).astype(BF)
        o, low, high = [], [], []
        for r in range(N):
            o.append(order(mx_ref.matmul(mx_ref.quantize(s[r]), now[r])))
            z = gcols(cut(d, r, 4 * n), o[r]).astype(np.float32).reshape(128, n // 2, 2, 4)
            low.append(half(z[:, :, 0] + z[:, :, 1]))
            high.append(half(z[:, :, 0] - z[:, :, 1]))
        orders.append(o)
        highs.append(high)
        low = swap(low, 1 << l, n // 2)
        now = [mx_ref.quantize(tile([mx_ref.matmul(pick(lay[r], np.arange(128 * b, 128 * b + 128)), low[r]) * np.float32(0.03125) for b in range(4)])) for r in range(N)]
    for l in (1, 0):
        m = C >> (l + 1)
        now = swap(now, 1 << l, m)
        d = decode(join(*now, *highs[l]))
        new = []
        for r in range(N):
            a, h = cut(d, r, 4 * m), cut(d, N + r, 4 * m)
            i = np.argsort(orders[l][r], axis=1)
            new.append(mx_ref.quantize(gcols(np.concatenate([(a + h).astype(BF), (a - h).astype(BF)], axis=1), i // 2 + m * (i % 2))))
        now = new
    y, ol = np.zeros((N, 128, C), np.float32), np.zeros((N, 8, C + C // 2), np.float32)
    oc, osc = np.zeros((N, 128, 4 * C), np.uint8), np.zeros((N, 16, C), np.uint8)
    for r in range(N):
        y[r] = mx_ref.matmul(mx_ref.quantize(v[r]), now[r])
        ol[r] = np.concatenate([orders[0][r], orders[1][r]], axis=1)
        oc[r], osc[r] = emit(now[r])
    return {"y": y, "ol": ol, "oc": oc, "osc": osc}

@@ -1,0 +1,479 @@
+from concourse.bass import DstId, RemoteDMATransfer
+from concourse.mybir import dt, AluOpType as A, ActivationFunctionType as F
+
+C = 384
+BIG = float(2 ** 80)
+B = 1024.0
+NS = (8, 4)
+SA = (10, 7)
+TOP = (4, 4)
+WHEN = ({10: (0,), 5: (3,), 3: (1,), 1: (4, 2), 0: (5,)}, {3: (0,), 1: (1,), 0: (2,)})
+EV = (1, 1, 0, 1, 0, 1, 0, 1)
+FW = (384, 320, 256, 192, 128, 128)
+
+S_, BF, F32, I32, U16, Q4, U8 = "sbuf", "bfloat16", "float32", "int32", "uint16", "float8_e4m3fn_x4", "uint8"
+SCRATCH = {"ps": ("psum", [128, 4096], F32)}
+for _n, _w, _d in [
+    ("tx", 1536, BF), ("tua", 512, BF), ("tub", 512, BF), ("tv", 512, BF),
+    ("ci", 8, I32), ("cf", 8, F32), ("cc", 12, F32), ("r16", 24, F32), ("t2", 384, BF), ("t4", 96, BF), ("jj", 384, F32), ("pki", 24, F32),
+    ("ones", 512, BF), ("sgA", 512, BF), ("sgB", 512, BF), ("ident", 128, BF), ("te", 2048, BF),
+    ("mM", 384, BF), ("mN", 384, BF), ("mN0", 384, BF), ("mR", 384, BF), ("m2", 384, BF), ("m4", 96, BF),
+    ("kk", 24, F32), ("pl", 8, U16), ("pkl", 20, U16), ("hl", 12, U16),
+    ("d1", 384, F32), ("px", 384, F32), ("rb", 384, BF), ("rs", 16 * 256, BF), ("rr0", 24, F32), ("rr1", 12, F32), ("xx", 24, F32),
+    ("sel", 384, F32),
+    ("iw0", 24, I32), ("iw1", 12, I32), ("iu", 24, U16), ("oo", 576, F32), ("sw", 384, F32), ("lw0", 96, U16), ("lw1", 48, U16),
+    ("sgn", 15 * 384, BF),
+    ("f0", 1536, BF), ("f1", 1280, BF), ("f2", 1024, BF), ("f3", 768, BF), ("f4", 512, BF), ("f5", 512, BF), ("f6", 768, BF),
+    ("dd0", 1536, BF), ("dd1", 768, BF), ("g30", 384, BF), ("g10", 384, BF), ("g31", 192, BF), ("g11", 192, BF),
+    ("lo", 512, BF), ("le", 512, BF), ("th0", 768, BF), ("ta1", 768, BF), ("tm", 576, BF), ("ta3", 768, BF), ("tf", 1536, BF),
+    ("w1", 1536, BF), ("w0", 1536, BF), ("ty", 384, F32),
+    ("z1", 24, I32), ("z2", 24, F32), ("z3", 24, F32), ("c0", 24, U16), ("lpar", 12, F32), ("lown", 12, F32), ("lland", 12, I32),
+    ("lmix", 12, I32), ("y1", 12, I32), ("y2", 12, F32), ("y3", 12, F32), ("c1", 12, U16),
+]:
+    SCRATCH[_n] = (S_, [128, _w], _d)
+for _n, _w in [("x", 384), ("ua", 128), ("ub", 128), ("v", 128), ("sa", 128), ("sb", 128), ("w2", 512), ("e", 512), ("en", 512), ("sg", 128),
+               ("f", 1408), ("lo0", 128), ("l0", 224), ("lo1", 128), ("l1", 176), ("h0", 192), ("h0n", 192), ("a1", 192), ("mo", 144),
+               ("m", 288), ("a2", 128), ("pk", 416), ("a3", 192), ("fin", 384)]:
+    SCRATCH["q" + _n] = (S_, [128, _w], Q4)
+    SCRATCH["s" + _n] = (S_, [128, _w], U8)
+
+SEMAPHORES = ["V", "S", "P", "G", "dx", "dx2", "dua", "dub", "dv", "dw", "sent", "a0", "a1", "am", "al", "a2", "og", "oh"]
+
+
+def rank_program(g, core, T, topo):
+    rank = T.rank_of(core)
+    if rank is None:
+        return
+    Q = {"V": g.vector, "S": g.scalar, "P": g.tensor, "G": g, "Y": g.sync}
+    cnt = {n: 0 for n in SEMAPHORES}
+    seen = {q: {} for q in Q}
+    lastw, readers = {}, {}
+    for n in SCRATCH:
+        w = SCRATCH[n][1][1]
+        lastw[n] = [None] * w
+        readers[n] = [None] * w
+
+    def v(n, a=0, b=None, s=1, ind=None):
+        return (n, a, SCRATCH[n][1][1] if b is None else b, s, ind)
+
+    def bank(k, a, b, s=1):
+        return v("ps", 512 * k + a, 512 * k + b, s)
+
+    def ap(x, cast=None):
+        n, a, b, s, ind = x
+        r = T[n][:, a:b] if s == 1 else T[n][:, a:b:s]
+        if cast is not None:
+            r = r.bitcast(cast)
+        if ind is not None:
+            r = r.indirect(ap(ind))
+        return r
+
+    def cols(x):
+        n, a, b, s, ind = x
+        if n == "ps":
+            return range(a // 512 * 512, a // 512 * 512 + 512, 512)
+        return range(a, b, s)
+
+    def need(q, reads, writes):
+        ev = {}
+
+        def add(e):
+            if e is not None and ev.get(e[0], 0) < e[1]:
+                ev[e[0]] = e[1]
+        for x in reads:
+            for c in cols(x):
+                add(lastw[x[0]][c])
+                if x[0] == "ps" and readers["ps"][c]:
+                    for s2, n2 in readers["ps"][c].items():
+                        if s2 != q:
+                            add((s2, n2))
+        for x in writes:
+            for c in cols(x):
+                e = lastw[x[0]][c]
+                if e is not None and not (e[0] == q == "P"):
+                    add(e)
+                if readers[x[0]][c]:
+                    for e in readers[x[0]][c].items():
+                        add(e)
+        for s2, n2 in ev.items():
+            if seen[q].get(s2, 0) < n2:
+                Q[q].wait_ge(T.sem[s2], n2)
+                seen[q][s2] = n2
+
+    def note(e, reads, writes):
+        for x in reads:
+            for c in cols(x):
+                if readers[x[0]][c] is None:
+                    readers[x[0]][c] = {}
+                readers[x[0]][c][e[0]] = e[1]
+        for x in writes:
+            for c in cols(x):
+                lastw[x[0]][c] = e
+                readers[x[0]][c] = None
+
+    def run(q, call, reads, writes):
+        reads = [x for x in reads if isinstance(x, tuple)]
+        reads = reads + [x[4] for x in reads + writes if x[4] is not None]
+        need(q, reads, writes)
+        cnt[q] += 1
+        call().then_inc(T.sem[q], 1)
+        note((q, cnt[q]), reads, writes)
+
+    def arg(x):
+        return ap(x) if isinstance(x, tuple) else x
+
+    def copy(o, i):
+        run("V", lambda: g.vector.tensor_copy(ap(o), ap(i)), [i], [o])
+
+    def tt(o, a, b, op):
+        run("V", lambda: g.vector.tensor_tensor(ap(o), ap(a), ap(b), op), [a, b], [o])
+
+    def ts(o, a, s1, op0, s2=None, op1=None):
+        if op1 is None:
+            run("V", lambda: g.vector.tensor_scalar(ap(o), ap(a), arg(s1), None, op0), [a, s1], [o])
+        else:
+            run("V", lambda: g.vector.tensor_scalar(ap(o), ap(a), arg(s1), arg(s2), op0, op1), [a, s1, s2], [o])
+
+    def scan(o, a, b, op0, op1):
+        run("V", lambda: g.vector.tensor_tensor_scan(ap(o), ap(a), ap(b), 0.0, op0, op1), [a, b], [o])
+
+    def mset(o, c):
+        run("V", lambda: g.vector.memset(ap(o), c), [], [o])
+
+    def act(o, i, fn, bias=None, scale=None, acc=None):
+        kw = {}
+        if bias is not None:
+            kw["bias"] = arg(bias)
+        if scale is not None:
+            kw["scale"] = arg(scale)
+        if acc is not None:
+            kw["accum_out"] = ap(acc)
+        run("S", lambda: g.scalar.activation(ap(o), ap(i), fn, **kw), [i, bias, scale], [o] + ([acc] if acc else []))
+
+    def move(q, o, i, scale=None):
+        if q == "S":
+            act(o, i, F.Copy, scale=scale)
+        elif scale is None:
+            copy(o, i)
+        else:
+            ts(o, i, scale, A.mult)
+
+    def quant(n, a, b, i):
+        run("V", lambda: g.vector.quantize_mx(ap(v("q" + n, a, b)), ap(v("s" + n, a, b)), ap(i)), [i], [v("q" + n, a, b), v("s" + n, a, b)])
+
+    def mm(k, w, wa, x, a, b, start=True, stop=True):
+        r = [v("q" + w, wa, wa + 128), v("s" + w, wa, wa + 128), v("q" + x, a, b), v("s" + x, a, b)]
+        o = bank(k, 0, b - a)
+        run("P", lambda: g.tensor.matmul_mx(ap(o), ap(r[0]), ap(r[1]), ap(r[2]), ap(r[3]), start, stop), r, [o])
+
+    def pick(o, a, b, src, lst):
+        oc_, ic = v("q" + o, a, b), v("q" + src, ind=lst)
+        run("V", lambda: g.vector.tensor_copy(ap(oc_, dt.uint32), ap(ic, dt.uint32)), [ic], [oc_])
+        act(v("s" + o, a, b), v("s" + src, ind=lst), F.Copy)
+
+    def iota(o, pat, base=0, cm=0):
+        if SCRATCH[o[0]][2] == I32:
+            run("G", lambda: g.iota(ap(o), pat, base, cm), [], [o])
+        else:
+            run("G", lambda: g.iota(ap(o), pat, base, cm, allow_small_or_imprecise_dtypes=True), [], [o])
+
+    def asel(o, i, pat, op, base, cm):
+        run("G", lambda: g.affine_select(ap(o), ap(i), pat, op, 0.0, base, cm), [i], [o])
+
+    def load(q, o, src, sem, cast=None):
+        need(q, [], [o])
+        cnt[sem] += 16
+        Q[q].dma_start(ap(o, cast), src).then_inc(T.sem[sem], 16)
+
+    def store(q, dst, src, i, sem):
+        need(q, [i], [])
+        cnt[sem] += 16
+        Q[q].dma_start(dst, src).then_inc(T.sem[sem], 16)
+
+    def send(parts):
+        need("G", [p[0] for p in parts], [])
+        trs = []
+        for k, (s, d, r, sem) in enumerate(parts):
+            dst = T.cores[r]
+            eng = topo.engines(core, dst)
+            share = len(eng) // len(parts)
+            mask = sum(1 << e for e in eng[k * share:(k + 1) * share])
+            cast = dt.uint8 if SCRATCH[s[0]][2] == Q4 else None
+            rid, pid = topo.addr(dst)[:2]
+            cnt["sent"] += share
+            cnt[sem] += share
+            if len(parts) == 1:
+                g.remote_dma(ap(d, cast), ap(s, cast), T.sem[sem], T.sem.sent, pid, rid, mask)
+            else:
+                trs.append(RemoteDMATransfer(dst_ids=[DstId(rid=rid, pnc=pid)], dma_engine_mask=mask, remote_sem=T.sem[sem],
+                                             src=ap(s, cast), dst=ap(d, cast)))
+        if trs:
+            g.remote_dma_fused(trs, local_sem=T.sem.sent)
+
+    def landed(views, sem):
+        note((sem, cnt[sem]), [], views)
+
+    def cf(k):
+        return v("cf", k, k + 1)
+
+    def cc(k):
+        return v("cc", k, k + 1)
+
+    def diagonals(sign):
+        for b in range(4):
+            act(v("te", 512 * b + b, 512 * b + 512, 4), v("ident"), F.Copy, scale=sign)
+
+    def pad(name, w, first):
+        iota(v(name, 4 * first, 4 * w), [[0, 4 * (w - first)]])
+
+    load("S", v("tua"), T.ua[:], "dua")
+    landed([v("tua")], "dua")
+    load("Y", v("tx", 0, 768), T.x[:, 0:768], "dx")
+    landed([v("tx", 0, 768)], "dx")
+    load("Y", v("tx", 768, 1536), T.x[:, 768:1536], "dx2")
+    landed([v("tx", 768, 1536)], "dx2")
+    iota(v("ci", 0, 1), [[0, 1]], 0, 1)
+    iota(v("r16"), [[16, 24]])
+    mset(v("ones"), 1.0)
+    mset(v("te", 0, 1024), 0.0)
+    asel(v("ident"), v("ones", 0, 128), [[-1, 128]], A.is_equal, 0, 1)
+    iota(v("t2"), [[0, 24], [2, 16]], -1)
+    for b in (2, 3):
+        act(v("te", 512 * b, 512 * b + 512), v("ones"), F.Copy, scale=0.0)
+    diagonals(1.0)
+    ts(v("ci", 1, 2), v("ci", 0, 1), 15, A.bitwise_and)
+    ts(v("ci", 2, 3), v("ci", 0, 1), 2, A.arith_shift_right, 3, A.bitwise_and)
+    ts(v("ci", 3, 4), v("ci", 0, 1), 3, A.bitwise_and)
+    ts(v("ci", 4, 5), v("ci", 0, 1), 1, A.bitwise_and)
+    ts(v("ci", 5, 6), v("ci", 0, 1), 1, A.arith_shift_right, 7, A.bitwise_and)
+    mset(cc(3), BIG)
+    copy(v("cf", 0, 6), v("ci", 0, 6))
+    mset(cc(4), 7.5 * B)
+    ts(cc(0), cf(1), 2.0, A.mult)
+    copy(v("pl"), v("r16", 0, 8))
+    ts(cc(1), cf(1), -(B + 1), A.mult, 15 * (B + 1), A.add)
+    ts(cc(8), cf(2), -4 * B, A.mult, 12 * B, A.add)
+    mset(v("rr0"), 0.0)
+    mset(v("rr1"), 0.0)
+    ts(v("mM"), v("t2"), cc(0), A.subtract, BIG, A.mult)
+    ts(v("mR"), v("t2"), 0.0, A.is_gt)
+    act(v("mN0"), v("mM"), F.Abs, bias=cc(3))
+    pad("f0", 384, 336)
+    asel(v("sgA"), v("ones"), [[-16, 8], [0, 64]], A.is_ge, 0, 1)
+    for u in (2, 3, 1):
+        pad("f%d" % u, FW[u], FW[u] - 48)
+    asel(v("sgB"), v("sgA"), [[16, 8], [0, 64]], A.is_ge, 15, -1)
+    pad("f4", 128, 80)
+    pad("f5", 128, 16)
+    iota(v("t4"), [[0, 24], [1, 4]])
+    iota(v("jj"), [[1, 384]])
+    pad("lo", 128, 96)
+    iota(v("le", 0, 128), [[0, 128]])
+    pad("f6", 192, 144)
+    iota(v("pki"), [[48, 4], [144, 2], [16, 3]])
+
+    quant("ua", 0, 128, v("tua"))
+    ts(v("kk"), v("r16"), cc(1), A.add)
+    pick("sa", 0, 128, "ua", v("pl"))
+    act(v("mN"), v("mN0"), F.Identity, bias=cc(3), scale=-1.0)
+    act(v("mN0"), v("mM"), F.Sign)
+    act(v("m2"), v("mN0"), F.Identity, bias=cc(4), scale=-8.5 * B)
+    ts(cc(2), cc(8), cf(3), A.add)
+    quant("e", 0, 256, v("te", 0, 1024))
+    quant("x", 0, 192, v("tx", 0, 768))
+    quant("x", 192, C, v("tx", 768, 1536))
+    need("Y", [v("tx")], [])
+    load("Y", v("qw2"), T.wc[:], "dw", dt.uint8)
+    load("Y", v("sw2"), T.ws[:], "dw")
+    landed([v("qw2"), v("sw2")], "dw")
+    load("Y", v("tub"), T.ub[:], "dub")
+    landed([v("tub")], "dub")
+    load("Y", v("tv"), T.v[:], "dv")
+    landed([v("tv")], "dv")
+
+    def down(l, s, a):
+        n = C >> l
+        nb, ns, h = n // 16, NS[l], n // 4
+        nv = nb - 1 - ns
+        tiles = ["f0", "f1", "f2", "f3", "f4", "f5"] if l == 0 else ["f6", "f4", "f5"]
+        wid = [SCRATCH[t][1][1] // 4 for t in tiles]
+        off = [sum(wid[:u]) for u in range(len(wid))]
+        oo, rr, sa = C * l, "rr%d" % l, SA[l]
+        iw, lw, dd, g3 = "iw%d" % l, "lw%d" % l, "dd%d" % l, "g3%d" % l
+
+        def slot(r, w):
+            k = nb - r
+            return v(tiles[k // 4], k % 4, 4 * w, 4)
+
+        def own(r):
+            return v("px", 16 * r + 15, 16 * r + 16)
+        mm(1, s, 0, a, 0, n)
+        mm(0, s, 0, a, 0, n)
+        if l == 0:
+            quant("e", 256, 512, v("te", 1024, 2048))
+        for b in range(4):
+            mm(4 + b, "e", 128 * b, a, 0, n)
+        top = 16 * (nb - TOP[l])
+        tt(v("d1", top, n), bank(1, top, n), v("mN", top, n), A.min)
+        scan(v("px", top, n), v("mM", top, n), v("d1", top, n), A.min, A.max)
+        tt(v("d1", 0, top), bank(0, 0, top), v("mN", 0, top), A.min)
+        scan(v("px", 0, top), v("mM", 0, top), v("d1", 0, top), A.min, A.max)
+        for k in range(ns + 1):
+            if k < ns:
+                r = nb - 1 - k
+                act(v("sgn", 384 * k, 384 * k + 16 * r), bank(1, 0, 16 * r), F.Sign, bias=own(r), scale=-1.0)
+            if k > 0:
+                r = nb - k
+                act(slot(r, 16 * r), v("sgn", 384 * (k - 1), 384 * (k - 1) + 16 * r), F.Relu, acc=v(rr, r, r + 1))
+        done = []
+
+        def sums(u):
+            if l == 0 and not done:
+                quant("sg", 0, 128, v("sgB"))
+            quant("f", off[u], off[u] + wid[u], v(tiles[u]))
+            mm(2, "sg", 0, "f", off[u], off[u] + wid[u], not done, len(done) == len(tiles) - 1)
+            done.append(u)
+        extra = {nv: lambda: tt(slot(nb, n), bank(0, 0, n), v("px", 0, n), A.is_le),
+                 nv - 1: lambda: scan(v("rb", 0, n), v("mR", 0, n), slot(nb, n), A.mult, A.add),
+                 nv - 2: lambda: tt(v("xx", 0, nb), v("kk", 0, nb), v("rb", 15, n, 16), A.subtract)}
+        for r in range(nv, -1, -1):
+            if r > 0:
+                ts(slot(r, 16 * r), bank(0, 0, 16 * r), own(r), A.is_lt)
+            if 0 < r <= sa:
+                act(v("sgn", 3456 + 160 * r, 3456 + 176 * r), slot(r, 16 * r), F.Identity, acc=v(rr, r, r + 1))
+            if sa <= r < nv:
+                scan(v("rs", 240 * r + 240, 256 * r + 256), v("ones", 0, 16 * r + 16), slot(r + 1, 16 * r + 16), A.mult, A.add)
+            if r in extra:
+                extra[r]()
+            for u in WHEN[l].get(r, ()):
+                sums(u)
+        if sa < nv:
+            tt(v("xx", sa + 1, nv + 1), v("xx", sa + 1, nv + 1), v("rs", 256 * sa + 255, 256 * nv, 256), A.subtract)
+        if l == 0:
+            ts(v("m4"), v("t4"), cf(2), A.is_le, 5 * B, A.mult)
+            ts(v("m4"), v("m4"), -B, A.add)
+        for b in range(4):
+            act(v(dd, b, 4 * n, 4), bank(4 + b, 0, n), F.Copy, scale=0.5)
+        scan(v("sel", 0, n), v("m2", 0, n), bank(2, 0, n), A.add, A.min)
+        tt(v("xx", 0, nb), v("xx", 0, nb), v(rr), A.subtract)
+        tt(v(iw), v("sel", 15, n, 16), v("xx", 0, nb), A.add)
+        copy(v("iu", 0, nb), v(iw))
+        if l == 1:
+            send([(v("iw1"), v("lland"), rank ^ 1, "al")])
+            landed([v("lland")], "al")
+        copy(v("oo", oo, oo + n, ind=v("iu", 0, nb)), v("jj", 0, n))
+        lists(l, 0)
+        move("S", v(g3, n // 2, n), v(dd, ind=v(lw, nb // 2, nb)))
+        move("V", v(g3, 0, n // 2), v(dd, ind=v(lw, 0, nb // 2)))
+        tt(v("lo", 0, n), v(dd, ind=v(lw, nb, 2 * nb)), v(g3), A.add)
+        quant("lo%d" % l, 0, 128, v("lo"))
+        p, land = rank ^ (1 << l), "l%d" % l
+        send([(v("qlo%d" % l, 0, h), v("q" + land, 128, 128 + h), p, "a%d" % l)])
+        send([(v("slo%d" % l, 0, h), v("s" + land, 128, 128 + h), p, "a%d" % l)])
+        landed([v("q" + land, 128, 128 + h), v("s" + land, 128, 128 + h)], "a%d" % l)
+        lists(l, 2)
+        move("S", v("g1%d" % l), v(dd, ind=v(lw, 2 * nb, 3 * nb)))
+
+    def lists(l, k0):
+        n = C >> l
+        h, nb, oo = n // 4, n // 16, C * l
+        for k in (k0, k0 + 1):
+            scan(v("sw", k * h, (k + 1) * h), v("m4", 0, h), v("oo", oo + 3 - k, oo + n, 4), A.add, A.min)
+        ts(v("lw%d" % l, k0 * nb, (k0 + 2) * nb), v("sw", k0 * h + 3, (k0 + 2) * h, 4), 4.0, A.mult, cc(2), A.add)
+
+    def layer(x, a, k0, h, out):
+        for b in range(4):
+            mm(k0 + b, "w2", 128 * b, x, a, a + 128)
+        for b in range(4):
+            move("VS"[b % 2], out(b), bank(k0 + b, 128 - h, 128), 0.03125)
+
+    def index(src, low, zi, zf, out):
+        ts(zi, src, low, A.bitwise_and)
+        ts(zf, zi, 383.0, A.mult)
+        tt(out, zf, src, A.add)
+
+    down(0, "sa", "x")
+    tt(v("th0", 0, 384), v("dd0", ind=v("lw0", 24, 48)), v("g30"), A.subtract)
+    quant("ub", 0, 128, v("tub"))
+    tt(v("le", 128, 512), v("dd0", ind=v("lw0", 72, 96)), v("g10"), A.add)
+    pick("sb", 0, 128, "ub", v("pl"))
+    diagonals(-1.0)
+    quant("l0", 0, 128, v("le"))
+    layer("l0", 0, 0, 96, lambda b: v("ta1", b, 768, 8))
+    layer("l0", 96, 4, 96, lambda b: v("ta1", 4 + b, 768, 8))
+    quant("a1", 0, 192, v("ta1"))
+
+    down(1, "sb", "a1")
+    store("Y", T.ol[:], T.oo[0:128:16, :], v("oo"), "oh")
+    tt(v("tm", 384, 576), v("dd1", ind=v("lw1", 12, 24)), v("g31"), A.subtract)
+    tt(v("le", 320, 512), v("dd1", ind=v("lw1", 36, 48)), v("g11"), A.add)
+    quant("l1", 0, 128, v("le"))
+    tt(v("tm", 192, 384), v("dd1", ind=v("lw1", 36, 48)), v("g11"), A.subtract)
+    layer("l1", 0, 0, 48, lambda b: v("tm", b, 192, 4))
+    quant("mo", 0, 144, v("tm"))
+    send([(v("qmo"), v("qm", 0, 144), rank ^ 1, "am")])
+    send([(v("smo"), v("sm", 0, 144), rank ^ 1, "am")])
+    landed([v("qm", 0, 144), v("sm", 0, 144)], "am")
+    index(v("iw0"), 1, v("z1"), v("z2"), v("z3"))
+    ts(v("c0"), v("z3"), 0.5, A.mult)
+    quant("en", 0, 512, v("te"))
+    layer("l1", 48, 4, 48, lambda b: v("lo", b, 192, 4))
+    quant("a2", 0, 128, v("lo"))
+    send([(v("qa2", 0, 48), v("qpk", 48, 96), rank ^ 2, "a2"), (v("qa2", 0, 48), v("qpk", 0, 48), rank ^ 3, "a2")])
+    send([(v("sa2", 0, 48), v("spk", 48, 96), rank ^ 2, "a2"), (v("sa2", 0, 48), v("spk", 0, 48), rank ^ 3, "a2")])
+    landed([v("qpk", 0, 96), v("spk", 0, 96)], "a2")
+
+    ts(cc(5), cf(4), -1.0, A.mult, 1.0, A.add)
+    ts(v("pkl"), v("pki", 0, 20), cf(1), A.add)
+    quant("m", 144, 288, v("tm"))
+    ts(cc(7), cc(5), 96.0, A.mult, cf(5), A.add)
+    tt(v("th0", 384, 768), v("dd0", ind=v("lw0", 72, 96)), v("g10"), A.subtract)
+    ts(v("hl"), v("r16", 0, 12), 0.5, A.mult, cc(7), A.add)
+    ts(v("lpar"), v("lland"), cf(4), A.mult)
+    ts(v("lown"), v("iw1"), cc(5), A.mult)
+    quant("h0", 0, 192, v("th0"))
+    tt(v("lmix"), v("lown"), v("lpar"), A.add)
+    pick("pk", 96, 416, "m", v("pkl"))
+    order = [(0, 0), (2, 0), (0, 1), (2, 1), (1, 0), (3, 0), (1, 1), (3, 1)]
+    sign = ("e", "en")
+    for k, (b, s) in enumerate(order):
+        mm(k, "e", 128 * b, "pk", 96, 224, True, False)
+        mm(k, sign[s], 128 * b, "pk", 192, 320, False, True)
+    ts(cc(6), cc(5), 48.0, A.mult)
+    index(v("lmix"), 3, v("y1"), v("y2"), v("y3"))
+    ts(v("c1"), v("y3"), 0.25, A.mult, cc(6), A.add)
+    for k, (b, s) in enumerate(order):
+        move("VS"[EV[k]], v("w1", 384 * b + 96 * s, 384 * b + 96 * s + 96), bank(k, 0, 96))
+        mm(k, sign[s], 128 * b, "pk", 288, 416, True, False)
+    for k, (b, s) in enumerate(order):
+        mm(k, "e", 128 * b, "pk", 0, 128, False, True)
+    pick("h0n", 0, 192, "h0", v("hl"))
+    for k, (b, s) in enumerate(order):
+        move("VS"[b // 2], v("w1", 384 * b + 192 + 96 * s, 384 * b + 288 + 96 * s), bank(k, 0, 96))
+    for b in (0, 2, 1, 3):
+        move("VS"[b // 2], v("ta3", b, 768, 4), v("w1", 384 * b, 384 * b + 384, ind=v("c1")))
+    for k, (b, s) in enumerate(order):
+        mm(k, sign[s], 128 * b, "h0n", 0, 192, True, False)
+    quant("a3", 0, 192, v("ta3"))
+    quant("v", 0, 128, v("tv"))
+
+    for k, (b, s) in enumerate(order):
+        mm(k, "e", 128 * b, "a3", 0, 192, False, True)
+    for k, (b, s) in enumerate(order):
+        move("VS"[b // 2], v("w0", 384 * b + 192 * s, 384 * b + 192 * s + 192), bank(k, 0, 192))
+    for b in (0, 2, 1, 3):
+        move("VS"[b // 2], v("tf", b, 1536, 4), v("w0", 384 * b, 384 * b + 384, ind=v("c0")))
+    quant("fin", 0, 192, v("tf", 0, 768))
+    mm(0, "v", 0, "fin", 0, 192)
+    quant("fin", 192, 384, v("tf", 768, 1536))
+    mm(1, "v", 0, "fin", 192, 384)
+    move("S", v("ty", 0, 192), bank(0, 0, 192))
+    move("V", v("ty", 192, 384), bank(1, 0, 192))
+    store("Y", T.oc[:], T.qfin[:].bitcast(dt.uint8), v("qfin"), "oh")
+    store("S", T.y[:, 0:192], T.ty[:, 0:192], v("ty", 0, 192), "oh")
+    for k in range(4):
+        store("YS"[k // 2], T.osc[4 * k:4 * k + 4, :], T.sfin[32 * k:32 * k + 4, :], v("sfin"), "oh")
+    store("Y", T.y[:, 192:384], T.ty[:, 192:384], v("ty", 192, 384), "oh")
+    for n in SEMAPHORES:
+        if cnt[n] and seen["G"].get(n, 0) < cnt[n]:
+            g.wait_ge(T.sem[n], cnt[n])

@@ -8,36 +8,36 @@ NS = (8, 4)
 SA = (10, 7)
 TOP = (4, 4)
 WHEN = ({10: (0,), 5: (3,), 3: (1,), 1: (4, 2), 0: (5,)}, {3: (0,), 1: (1,), 0: (2,)})
-EV = (1, 1, 0, 1, 0, 1, 0, 1)
+CUT = 256
 FW = (384, 320, 256, 192, 128, 128)
 
 S_, BF, F32, I32, U16, Q4, U8 = "sbuf", "bfloat16", "float32", "int32", "uint16", "float8_e4m3fn_x4", "uint8"
 SCRATCH = {"ps": ("psum", [128, 4096], F32)}
 for _n, _w, _d in [
     ("tx", 1536, BF), ("tua", 512, BF), ("tub", 512, BF), ("tv", 512, BF),
-    ("ci", 8, I32), ("cf", 8, F32), ("cc", 12, F32), ("r16", 24, F32), ("t2", 384, BF), ("t4", 96, BF), ("jj", 384, F32), ("pki", 24, F32),
-    ("ones", 512, BF), ("sgA", 512, BF), ("sgB", 512, BF), ("ident", 128, BF), ("te", 2048, BF),
+    ("ci", 8, I32), ("cf", 8, F32), ("cc", 12, F32), ("r16", 24, F32), ("t2", 384, BF), ("t4", 96, BF), ("jj", 384, F32),
+    ("ones", 514, BF), ("sgA", 512, BF), ("sgB", 512, BF), ("e0", 514, BF), ("e1", 514, BF), ("en0", 514, BF), ("en1", 514, BF),
     ("mM", 384, BF), ("mN", 384, BF), ("mN0", 384, BF), ("mR", 384, BF), ("m2", 384, BF), ("m4", 96, BF),
-    ("kk", 24, F32), ("pl", 8, U16), ("pkl", 20, U16), ("hl", 12, U16),
+    ("kk", 24, F32), ("pl", 8, U16), ("hl", 12, U16),
     ("d1", 384, F32), ("px", 384, F32), ("rb", 384, BF), ("rs", 16 * 256, BF), ("rr0", 24, F32), ("rr1", 12, F32), ("xx", 24, F32),
     ("sel", 384, F32),
     ("iw0", 24, I32), ("iw1", 12, I32), ("iu", 24, U16), ("oo", 576, F32), ("sw", 384, F32), ("lw0", 96, U16), ("lw1", 48, U16),
     ("sgn", 15 * 384, BF),
     ("f0", 1536, BF), ("f1", 1280, BF), ("f2", 1024, BF), ("f3", 768, BF), ("f4", 512, BF), ("f5", 512, BF), ("f6", 768, BF),
     ("dd0", 1536, BF), ("dd1", 768, BF), ("g30", 384, BF), ("g10", 384, BF), ("g31", 192, BF), ("g11", 192, BF),
-    ("lo", 512, BF), ("le", 512, BF), ("th0", 768, BF), ("ta1", 768, BF), ("tm", 576, BF), ("ta3", 768, BF), ("tf", 1536, BF),
+    ("lo", 512, BF), ("le", 512, BF), ("th0", 768, BF), ("ta1", 768, BF), ("tm", 512, BF), ("th1", 512, BF), ("ta3", 768, BF), ("tf", 1536, BF),
     ("w1", 1536, BF), ("w0", 1536, BF), ("ty", 384, F32),
     ("z1", 24, I32), ("z2", 24, F32), ("z3", 24, F32), ("c0", 24, U16), ("lpar", 12, F32), ("lown", 12, F32), ("lland", 12, I32),
-    ("lmix", 12, I32), ("y1", 12, I32), ("y2", 12, F32), ("y3", 12, F32), ("c1", 12, U16),
+    ("lmix", 12, I32), ("yi", 24, I32), ("yf", 48, F32), ("c1", 12, U16),
 ]:
     SCRATCH[_n] = (S_, [128, _w], _d)
 for _n, _w in [("x", 384), ("ua", 128), ("ub", 128), ("v", 128), ("sa", 128), ("sb", 128), ("w2", 512), ("e", 512), ("en", 512), ("sg", 128),
-               ("f", 1408), ("lo0", 128), ("l0", 224), ("lo1", 128), ("l1", 176), ("h0", 192), ("h0n", 192), ("a1", 192), ("mo", 144),
-               ("m", 288), ("a2", 128), ("pk", 416), ("a3", 192), ("fin", 384)]:
+               ("f", 1408), ("lo0", 128), ("l0", 224), ("lo1", 128), ("l1", 176), ("h0", 192), ("h0n", 192), ("a1", 192), ("hh", 224),
+               ("st", 272), ("a2", 128), ("a3", 192), ("fin", 384)]:
     SCRATCH["q" + _n] = (S_, [128, _w], Q4)
     SCRATCH["s" + _n] = (S_, [128, _w], U8)
 
-SEMAPHORES = ["V", "S", "P", "G", "dx", "dx2", "dua", "dub", "dv", "dw", "sent", "a0", "a1", "am", "al", "a2", "og", "oh"]
+SEMAPHORES = ["V", "S", "P", "G", "dx", "dx2", "dua", "dub", "dv", "dw", "sent", "a0", "a1", "am", "ah", "al", "a2", "oh"]
 
 
 def rank_program(g, core, T, topo):
@@ -213,15 +213,20 @@ def rank_program(g, core, T, topo):
     def landed(views, sem):
         note((sem, cnt[sem]), [], views)
 
+    def cross(n, a, w, dests, sem):
+        for t in "qs":
+            send([(v(t + n, a, a + w), v(t + d, c, c + w), r, sem) for d, c, r in dests])
+        landed([v(t + d, c, c + w) for d, c, r in dests for t in "qs"], sem)
+
     def cf(k):
         return v("cf", k, k + 1)
 
     def cc(k):
         return v("cc", k, k + 1)
 
-    def diagonals(sign):
-        for b in range(4):
-            act(v("te", 512 * b + b, 512 * b + 512, 4), v("ident"), F.Copy, scale=sign)
+    def unit(n, b):
+        a = 2 - (b & 2)
+        quant(n, 128 * b, 128 * b + 128, v("%s%d" % (n, b & 1), a, a + 512))
 
     def pad(name, w, first):
         iota(v(name, 4 * first, 4 * w), [[0, 4 * (w - first)]])
@@ -233,55 +238,47 @@ def rank_program(g, core, T, topo):
     load("Y", v("tx", 768, 1536), T.x[:, 768:1536], "dx2")
     landed([v("tx", 768, 1536)], "dx2")
     iota(v("ci", 0, 1), [[0, 1]], 0, 1)
+    iota(v("ci", 6, 7), [[0, 1]], 0, 2)
     iota(v("r16"), [[16, 24]])
-    mset(v("ones"), 1.0)
-    mset(v("te", 0, 1024), 0.0)
-    asel(v("ident"), v("ones", 0, 128), [[-1, 128]], A.is_equal, 0, 1)
     iota(v("t2"), [[0, 24], [2, 16]], -1)
-    for b in (2, 3):
-        act(v("te", 512 * b, 512 * b + 512), v("ones"), F.Copy, scale=0.0)
-    diagonals(1.0)
-    ts(v("ci", 1, 2), v("ci", 0, 1), 15, A.bitwise_and)
+    mset(v("ones"), 1.0)
+    mset(cc(3), BIG)
     ts(v("ci", 2, 3), v("ci", 0, 1), 2, A.arith_shift_right, 3, A.bitwise_and)
     ts(v("ci", 3, 4), v("ci", 0, 1), 3, A.bitwise_and)
-    ts(v("ci", 4, 5), v("ci", 0, 1), 1, A.bitwise_and)
-    ts(v("ci", 5, 6), v("ci", 0, 1), 1, A.arith_shift_right, 7, A.bitwise_and)
-    mset(cc(3), BIG)
-    copy(v("cf", 0, 6), v("ci", 0, 6))
-    mset(cc(4), 7.5 * B)
-    ts(cc(0), cf(1), 2.0, A.mult)
+    ts(v("ci", 1, 2), v("ci", 6, 7), 31, A.bitwise_and)
     copy(v("pl"), v("r16", 0, 8))
-    ts(cc(1), cf(1), -(B + 1), A.mult, 15 * (B + 1), A.add)
+    copy(v("cf", 1, 4), v("ci", 1, 4))
+    act(v("rr0"), v("r16"), F.Copy, scale=0.0)
+    act(v("rr1"), v("r16", 0, 12), F.Copy, scale=0.0)
+    ts(cc(1), cf(1), (B - 1) / 2, A.mult, 15 * (1 - B), A.add)
     ts(cc(8), cf(2), -4 * B, A.mult, 12 * B, A.add)
-    mset(v("rr0"), 0.0)
-    mset(v("rr1"), 0.0)
-    ts(v("mM"), v("t2"), cc(0), A.subtract, BIG, A.mult)
-    ts(v("mR"), v("t2"), 0.0, A.is_gt)
+    ts(v("mM"), v("t2"), cf(1), A.subtract, BIG, A.mult)
     act(v("mN0"), v("mM"), F.Abs, bias=cc(3))
-    pad("f0", 384, 336)
-    asel(v("sgA"), v("ones"), [[-16, 8], [0, 64]], A.is_ge, 0, 1)
-    for u in (2, 3, 1):
+    for u in (0, 2, 3):
         pad("f%d" % u, FW[u], FW[u] - 48)
-    asel(v("sgB"), v("sgA"), [[16, 8], [0, 64]], A.is_ge, 15, -1)
+    iota(v("t4"), [[0, 24], [1, 4]])
+    pad("f1", FW[1], FW[1] - 48)
     pad("f4", 128, 80)
     pad("f5", 128, 16)
-    iota(v("t4"), [[0, 24], [1, 4]])
+    asel(v("sgA"), v("ones", 0, 512), [[-16, 8], [0, 64]], A.is_ge, 0, 1)
+    asel(v("sgB"), v("sgA"), [[16, 8], [0, 64]], A.is_ge, 15, -1)
+    for u in range(2):
+        asel(v("e%d" % u), v("ones"), [[1, 514]], A.is_equal, -2 - u, -4)
     iota(v("jj"), [[1, 384]])
     pad("lo", 128, 96)
     iota(v("le", 0, 128), [[0, 128]])
     pad("f6", 192, 144)
-    iota(v("pki"), [[48, 4], [144, 2], [16, 3]])
+    iota(v("th1", 0, 128), [[0, 128]])
+    iota(v("tm", 0, 320), [[0, 320]])
 
     quant("ua", 0, 128, v("tua"))
     ts(v("kk"), v("r16"), cc(1), A.add)
     pick("sa", 0, 128, "ua", v("pl"))
     act(v("mN"), v("mN0"), F.Identity, bias=cc(3), scale=-1.0)
-    act(v("mN0"), v("mM"), F.Sign)
-    act(v("m2"), v("mN0"), F.Identity, bias=cc(4), scale=-8.5 * B)
-    ts(cc(2), cc(8), cf(3), A.add)
-    quant("e", 0, 256, v("te", 0, 1024))
     quant("x", 0, 192, v("tx", 0, 768))
     quant("x", 192, C, v("tx", 768, 1536))
+    ts(v("mR"), v("t2"), 0.0, A.is_gt)
+    ts(v("m2"), v("mM"), -16 * B, A.max, B, A.min)
     need("Y", [v("tx")], [])
     load("Y", v("qw2"), T.wc[:], "dw", dt.uint8)
     load("Y", v("sw2"), T.ws[:], "dw")
@@ -290,6 +287,12 @@ def rank_program(g, core, T, topo):
     landed([v("tub")], "dub")
     load("Y", v("tv"), T.v[:], "dv")
     landed([v("tv")], "dv")
+
+    fill = []
+
+    def idle(k):
+        for _ in range(min(k, len(fill))):
+            fill.pop(0)()
 
     def down(l, s, a):
         n = C >> l
@@ -307,16 +310,32 @@ def rank_program(g, core, T, topo):
 
         def own(r):
             return v("px", 16 * r + 15, 16 * r + 16)
+
+        def unpack(b):
+            if l == 0:
+                unit("e", b)
+            mm(4 + b, "e", 128 * b, a, 0, n)
+
+        def halve(b):
+            act(v(dd, b, 4 * n, 4), bank(4 + b, 0, n), F.Copy, scale=0.5)
+
+        def evens():
+            lists(l, 2)
+            move("S", v("g1%d" % l), v(dd, ind=v(lw, 2 * nb, 3 * nb)))
         mm(1, s, 0, a, 0, n)
         mm(0, s, 0, a, 0, n)
-        if l == 0:
-            quant("e", 256, 512, v("te", 1024, 2048))
-        for b in range(4):
-            mm(4 + b, "e", 128 * b, a, 0, n)
+        if l == 1:
+            for b in range(4):
+                unpack(b)
+        idle(2)
         top = 16 * (nb - TOP[l])
         tt(v("d1", top, n), bank(1, top, n), v("mN", top, n), A.min)
+        if l == 0:
+            ts(cc(2), cc(8), cf(3), A.add)
         scan(v("px", top, n), v("mM", top, n), v("d1", top, n), A.min, A.max)
         tt(v("d1", 0, top), bank(0, 0, top), v("mN", 0, top), A.min)
+        if l == 0:
+            ts(v("m4"), v("t4"), cf(2), A.is_le, 5 * B, A.mult)
         scan(v("px", 0, top), v("mM", 0, top), v("d1", 0, top), A.min, A.max)
         for k in range(ns + 1):
             if k < ns:
@@ -345,34 +364,49 @@ def rank_program(g, core, T, topo):
                 scan(v("rs", 240 * r + 240, 256 * r + 256), v("ones", 0, 16 * r + 16), slot(r + 1, 16 * r + 16), A.mult, A.add)
             if r in extra:
                 extra[r]()
+            if r == 3:
+                idle(2)
             for u in WHEN[l].get(r, ()):
                 sums(u)
         if sa < nv:
             tt(v("xx", sa + 1, nv + 1), v("xx", sa + 1, nv + 1), v("rs", 256 * sa + 255, 256 * nv, 256), A.subtract)
+        idle(3)
         if l == 0:
-            ts(v("m4"), v("t4"), cf(2), A.is_le, 5 * B, A.mult)
-            ts(v("m4"), v("m4"), -B, A.add)
-        for b in range(4):
-            act(v(dd, b, 4 * n, 4), bank(4 + b, 0, n), F.Copy, scale=0.5)
-        scan(v("sel", 0, n), v("m2", 0, n), bank(2, 0, n), A.add, A.min)
+            unpack(0)
+            unpack(2)
+        for b in (0, 2) if l == 0 else range(4):
+            halve(b)
+        scan(v("sel", 0, n), v("m2", 0, n), bank(2, 0, n), A.add, A.max)
         tt(v("xx", 0, nb), v("xx", 0, nb), v(rr), A.subtract)
+        if l == 0:
+            unpack(1)
+            halve(1)
+        idle(1)
         tt(v(iw), v("sel", 15, n, 16), v("xx", 0, nb), A.add)
+        if l == 0:
+            unpack(3)
+            halve(3)
+        idle(1)
         copy(v("iu", 0, nb), v(iw))
+        idle(1)
+        if l == 0:
+            ts(v("m4"), v("m4"), -B, A.add)
         if l == 1:
             send([(v("iw1"), v("lland"), rank ^ 1, "al")])
             landed([v("lland")], "al")
         copy(v("oo", oo, oo + n, ind=v("iu", 0, nb)), v("jj", 0, n))
         lists(l, 0)
-        move("S", v(g3, n // 2, n), v(dd, ind=v(lw, nb // 2, nb)))
-        move("V", v(g3, 0, n // 2), v(dd, ind=v(lw, 0, nb // 2)))
+        if l == 0:
+            move("S", v(g3, n // 2, n), v(dd, ind=v(lw, nb // 2, nb)))
+            move("V", v(g3, 0, n // 2), v(dd, ind=v(lw, 0, nb // 2)))
+        else:
+            move("S", v(g3), v(dd, ind=v(lw, 0, nb)))
+            evens()
         tt(v("lo", 0, n), v(dd, ind=v(lw, nb, 2 * nb)), v(g3), A.add)
         quant("lo%d" % l, 0, 128, v("lo"))
-        p, land = rank ^ (1 << l), "l%d" % l
-        send([(v("qlo%d" % l, 0, h), v("q" + land, 128, 128 + h), p, "a%d" % l)])
-        send([(v("slo%d" % l, 0, h), v("s" + land, 128, 128 + h), p, "a%d" % l)])
-        landed([v("q" + land, 128, 128 + h), v("s" + land, 128, 128 + h)], "a%d" % l)
-        lists(l, 2)
-        move("S", v("g1%d" % l), v(dd, ind=v(lw, 2 * nb, 3 * nb)))
+        cross("lo%d" % l, 0, h, [("l%d" % l, 128, rank ^ (1 << l))], "a%d" % l)
+        if l == 0:
+            evens()
 
     def lists(l, k0):
         n = C >> l
@@ -381,99 +415,111 @@ def rank_program(g, core, T, topo):
             scan(v("sw", k * h, (k + 1) * h), v("m4", 0, h), v("oo", oo + 3 - k, oo + n, 4), A.add, A.min)
         ts(v("lw%d" % l, k0 * nb, (k0 + 2) * nb), v("sw", k0 * h + 3, (k0 + 2) * h, 4), 4.0, A.mult, cc(2), A.add)
 
-    def layer(x, a, k0, h, out):
+    def layer(x, a, k0, h, out, who="VSVS"):
         for b in range(4):
             mm(k0 + b, "w2", 128 * b, x, a, a + 128)
         for b in range(4):
-            move("VS"[b % 2], out(b), bank(k0 + b, 128 - h, 128), 0.03125)
-
-    def index(src, low, zi, zf, out):
-        ts(zi, src, low, A.bitwise_and)
-        ts(zf, zi, 383.0, A.mult)
-        tt(out, zf, src, A.add)
+            move(who[b], out(b), bank(k0 + b, 128 - h, 128), 0.03125)
 
     down(0, "sa", "x")
     tt(v("th0", 0, 384), v("dd0", ind=v("lw0", 24, 48)), v("g30"), A.subtract)
     quant("ub", 0, 128, v("tub"))
     tt(v("le", 128, 512), v("dd0", ind=v("lw0", 72, 96)), v("g10"), A.add)
     pick("sb", 0, 128, "ub", v("pl"))
-    diagonals(-1.0)
+    for u in range(2):
+        act(v("en%d" % u), v("e%d" % u), F.Copy, scale=-1.0)
     quant("l0", 0, 128, v("le"))
-    layer("l0", 0, 0, 96, lambda b: v("ta1", b, 768, 8))
+    ts(v("ci", 4, 5), v("ci", 0, 1), 1, A.bitwise_and)
+    ts(v("ci", 5, 6), v("ci", 0, 1), 1, A.arith_shift_right, 7, A.bitwise_and)
+    layer("l0", 0, 0, 96, lambda b: v("ta1", b, 768, 8), "SSSS")
+    copy(v("cf", 4, 6), v("ci", 4, 6))
+    unit("en", 0)
+    unit("en", 2)
     layer("l0", 96, 4, 96, lambda b: v("ta1", 4 + b, 768, 8))
     quant("a1", 0, 192, v("ta1"))
+    fill.extend([lambda: unit("en", 1), lambda: unit("en", 3),
+                 lambda: ts(v("z1"), v("iw0"), 1, A.bitwise_and),
+                 lambda: ts(cc(5), cf(4), -1.0, A.mult, 1.0, A.add),
+                 lambda: ts(v("z2"), v("z1"), 383.0, A.mult),
+                 lambda: ts(cc(7), cc(5), 96.0, A.mult, cf(5), A.add),
+                 lambda: tt(v("z3"), v("z2"), v("iw0"), A.add),
+                 lambda: ts(cc(6), cf(4), 96.0, A.mult),
+                 lambda: ts(v("hl"), v("r16", 0, 12), 0.5, A.mult, cc(7), A.add),
+                 lambda: ts(v("c0"), v("z3"), 0.5, A.mult)])
 
     down(1, "sb", "a1")
+    idle(len(fill))
     store("Y", T.ol[:], T.oo[0:128:16, :], v("oo"), "oh")
-    tt(v("tm", 384, 576), v("dd1", ind=v("lw1", 12, 24)), v("g31"), A.subtract)
     tt(v("le", 320, 512), v("dd1", ind=v("lw1", 36, 48)), v("g11"), A.add)
+    tt(v("th1", 320, 512), v("dd1", ind=v("lw1", 12, 24)), v("g31"), A.subtract)
     quant("l1", 0, 128, v("le"))
-    tt(v("tm", 192, 384), v("dd1", ind=v("lw1", 36, 48)), v("g11"), A.subtract)
-    layer("l1", 0, 0, 48, lambda b: v("tm", b, 192, 4))
-    quant("mo", 0, 144, v("tm"))
-    send([(v("qmo"), v("qm", 0, 144), rank ^ 1, "am")])
-    send([(v("smo"), v("sm", 0, 144), rank ^ 1, "am")])
-    landed([v("qm", 0, 144), v("sm", 0, 144)], "am")
-    index(v("iw0"), 1, v("z1"), v("z2"), v("z3"))
-    ts(v("c0"), v("z3"), 0.5, A.mult)
-    quant("en", 0, 512, v("te"))
+    tt(v("th1", 128, 320), v("dd1", ind=v("lw1", 36, 48)), v("g11"), A.subtract)
+    for b in range(4):
+        mm(b, "w2", 128 * b, "l1", 0, 128)
+    quant("hh", 0, 128, v("th1"))
+    cross("hh", 32, 96, [("hh", 128, rank ^ 1)], "ah")
+    for b in range(4):
+        move("SSVS"[b], v("tm", 320 + b, 512, 4), bank(b, 80, 128), 0.03125)
+    quant("st", 0, 128, v("tm"))
+    cross("st", 80, 48, [("st", 176, rank ^ 1)], "am")
     layer("l1", 48, 4, 48, lambda b: v("lo", b, 192, 4))
     quant("a2", 0, 128, v("lo"))
-    send([(v("qa2", 0, 48), v("qpk", 48, 96), rank ^ 2, "a2"), (v("qa2", 0, 48), v("qpk", 0, 48), rank ^ 3, "a2")])
-    send([(v("sa2", 0, 48), v("spk", 48, 96), rank ^ 2, "a2"), (v("sa2", 0, 48), v("spk", 0, 48), rank ^ 3, "a2")])
-    landed([v("qpk", 0, 96), v("spk", 0, 96)], "a2")
+    cross("a2", 0, 48, [("st", 128, rank ^ 2), ("st", 224, rank ^ 3)], "a2")
 
-    ts(cc(5), cf(4), -1.0, A.mult, 1.0, A.add)
-    ts(v("pkl"), v("pki", 0, 20), cf(1), A.add)
-    quant("m", 144, 288, v("tm"))
-    ts(cc(7), cc(5), 96.0, A.mult, cf(5), A.add)
+    order = [(0, 0), (2, 0), (0, 1), (2, 1), (1, 0), (3, 0), (1, 1), (3, 1)]
+    sign = ("e", "en")
+    for k, (b, s) in enumerate(order):
+        mm(k, sign[s], 128 * b, "hh", 32, 224, True, False)
     tt(v("th0", 384, 768), v("dd0", ind=v("lw0", 72, 96)), v("g10"), A.subtract)
-    ts(v("hl"), v("r16", 0, 12), 0.5, A.mult, cc(7), A.add)
     ts(v("lpar"), v("lland"), cf(4), A.mult)
     ts(v("lown"), v("iw1"), cc(5), A.mult)
     quant("h0", 0, 192, v("th0"))
     tt(v("lmix"), v("lown"), v("lpar"), A.add)
-    pick("pk", 96, 416, "m", v("pkl"))
-    order = [(0, 0), (2, 0), (0, 1), (2, 1), (1, 0), (3, 0), (1, 1), (3, 1)]
-    sign = ("e", "en")
-    for k, (b, s) in enumerate(order):
-        mm(k, "e", 128 * b, "pk", 96, 224, True, False)
-        mm(k, sign[s], 128 * b, "pk", 192, 320, False, True)
-    ts(cc(6), cc(5), 48.0, A.mult)
-    index(v("lmix"), 3, v("y1"), v("y2"), v("y3"))
-    ts(v("c1"), v("y3"), 0.25, A.mult, cc(6), A.add)
-    for k, (b, s) in enumerate(order):
-        move("VS"[EV[k]], v("w1", 384 * b + 96 * s, 384 * b + 96 * s + 96), bank(k, 0, 96))
-        mm(k, sign[s], 128 * b, "pk", 288, 416, True, False)
-    for k, (b, s) in enumerate(order):
-        mm(k, "e", 128 * b, "pk", 0, 128, False, True)
     pick("h0n", 0, 192, "h0", v("hl"))
+    ts(v("yi", 0, 12), v("lmix"), 1, A.bitwise_and)
+    ts(v("yi", 12, 24), v("lmix"), 2, A.bitwise_and)
+    ts(v("yf", 0, 12), v("yi", 0, 12), 767.0, A.mult)
+    ts(v("yf", 24, 36), v("yi", 12, 24), 95.0, A.mult)
+    tt(v("yf", 12, 24), v("yf", 0, 12), v("lmix"), A.add)
+    quant("v", 0, 128, v("tv"))
+    tt(v("yf", 36, 48), v("yf", 12, 24), v("yf", 24, 36), A.add)
+    ts(v("c1"), v("yf", 36, 48), 0.25, A.mult, cc(6), A.add)
     for k, (b, s) in enumerate(order):
-        move("VS"[b // 2], v("w1", 384 * b + 192 + 96 * s, 384 * b + 288 + 96 * s), bank(k, 0, 96))
+        mm(k, "e", 128 * b, "st", 80, 272, False, True)
+    for k, (b, s) in enumerate(order):
+        move("VS"[b // 2], v("w1", 384 * b + 192 * s, 384 * b + 192 * s + 192), bank(k, 0, 192))
     for b in (0, 2, 1, 3):
         move("VS"[b // 2], v("ta3", b, 768, 4), v("w1", 384 * b, 384 * b + 384, ind=v("c1")))
     for k, (b, s) in enumerate(order):
         mm(k, sign[s], 128 * b, "h0n", 0, 192, True, False)
     quant("a3", 0, 192, v("ta3"))
-    quant("v", 0, 128, v("tv"))
 
     for k, (b, s) in enumerate(order):
         mm(k, "e", 128 * b, "a3", 0, 192, False, True)
     for k, (b, s) in enumerate(order):
         move("VS"[b // 2], v("w0", 384 * b + 192 * s, 384 * b + 192 * s + 192), bank(k, 0, 192))
+
+    def back(b, a, e):
+        move("VS"[b // 2], v("tf", 4 * a + b, 4 * e, 4), v("w0", 384 * b, 384 * b + 384, ind=v("c0", a // 16, e // 16)))
+
+    def finish(k, a, e):
+        quant("fin", a, e, v("tf", 4 * a, 4 * e))
+        mm(k, "v", 0, "fin", a, e)
+        store("Y", T.oc[:, 4 * a:4 * e], T.qfin[:, a:e].bitcast(dt.uint8), v("qfin", a, e), "oh")
     for b in (0, 2, 1, 3):
-        move("VS"[b // 2], v("tf", b, 1536, 4), v("w0", 384 * b, 384 * b + 384, ind=v("c0")))
-    quant("fin", 0, 192, v("tf", 0, 768))
-    mm(0, "v", 0, "fin", 0, 192)
-    quant("fin", 192, 384, v("tf", 768, 1536))
-    mm(1, "v", 0, "fin", 192, 384)
-    move("S", v("ty", 0, 192), bank(0, 0, 192))
-    move("V", v("ty", 192, 384), bank(1, 0, 192))
-    store("Y", T.oc[:], T.qfin[:].bitcast(dt.uint8), v("qfin"), "oh")
-    store("S", T.y[:, 0:192], T.ty[:, 0:192], v("ty", 0, 192), "oh")
+        back(b, 0, CUT)
+    back(2, CUT, C)
+    finish(0, 0, CUT)
+    back(0, CUT, C)
+    back(3, CUT, C)
+    back(1, CUT, C)
+    move("S", v("ty", 0, CUT), bank(0, 0, CUT))
+    finish(1, CUT, C)
+    move("V", v("ty", CUT, C), bank(1, 0, C - CUT))
+    store("S", T.y[:, 0:CUT], T.ty[:, 0:CUT], v("ty", 0, CUT), "oh")
     for k in range(4):
-        store("YS"[k // 2], T.osc[4 * k:4 * k + 4, :], T.sfin[32 * k:32 * k + 4, :], v("sfin"), "oh")
-    store("Y", T.y[:, 192:384], T.ty[:, 192:384], v("ty", 192, 384), "oh")
+        store("Y", T.osc[4 * k:4 * k + 4, :], T.sfin[32 * k:32 * k + 4, :], v("sfin"), "oh")
+    store("S", T.y[:, CUT:C], T.ty[:, CUT:C], v("ty", CUT, C), "oh")
     for n in SEMAPHORES:
         if cnt[n] and seen["G"].get(n, 0) < cnt[n]:
             g.wait_ge(T.sem[n], cnt[n])

@@ -4,40 +4,37 @@ from concourse.mybir import dt, AluOpType as A, ActivationFunctionType as F
 C = 384
 BIG = float(2 ** 80)
 B = 1024.0
-NS = (8, 4)
-SA = (10, 7)
-TOP = (4, 4)
-WHEN = ({10: (0,), 5: (3,), 3: (1,), 1: (4, 2), 0: (5,)}, {3: (0,), 1: (1,), 0: (2,)})
+SR = ((23, 22, 21, 20, 19, 18, 17), (11, 10, 9))
+VR = (("e0", "e2", "o320", "e1", "s", "e3", "o0", "R", "s", "S", 16, "d", 15, 14, "r16", "b", 13, "r15", 12, "r14", "k", 11, "r13", 10, "r12",
+       9, "r11", "g", "q0", 8, "r10", 7, "r9", 6, "r8", 5, "r7", "q3", 4, "r6", 3, "r5", "q4", 2, "r4", 1, "r3", "q2", "q1", "r2", "q5", "r1",
+       "w", "v"),
+      ("i", "o128", "s", "o0", "s", "S", 8, "d", 7, 6, "r8", "b", 5, "r7", 4, "r6", "k", 3, "r5", 2, "r4", 1, "q0", "q1", "r3", "r2", "q2",
+       "r1", "w", "v"))
+TAIL = ("S00", "S10", "S20", "V30", "V01", "f0", "S11", "S21", "V31", "y", "f1")
 CUT = 256
 FW = (384, 320, 256, 192, 128, 128)
+FIRST = (336, 272, 208, 144, 80, 16)
 
 S_, BF, F32, I32, U16, Q4, U8 = "sbuf", "bfloat16", "float32", "int32", "uint16", "float8_e4m3fn_x4", "uint8"
 SCRATCH = {"ps": ("psum", [128, 4096], F32)}
-for _n, _w, _d in [
-    ("tx", 1536, BF), ("tua", 512, BF), ("tub", 512, BF), ("tv", 512, BF),
-    ("ci", 8, I32), ("cf", 8, F32), ("cc", 12, F32), ("r16", 24, F32), ("t2", 384, BF), ("t4", 96, BF), ("jj", 384, F32),
-    ("ones", 514, BF), ("sgA", 512, BF), ("sgB", 512, BF), ("e0", 514, BF), ("e1", 514, BF), ("en0", 514, BF), ("en1", 514, BF),
-    ("mM", 384, BF), ("mN", 384, BF), ("mN0", 384, BF), ("mR", 384, BF), ("m2", 384, BF), ("m4", 96, BF),
-    ("kk", 24, F32), ("pl", 8, U16), ("hl", 12, U16),
-    ("d1", 384, F32), ("px", 384, F32), ("rb", 384, BF), ("rs", 16 * 256, BF), ("rr0", 24, F32), ("rr1", 12, F32), ("xx", 24, F32),
-    ("sel", 384, F32),
-    ("iw0", 24, I32), ("iw1", 12, I32), ("iu", 24, U16), ("oo", 576, F32), ("sw", 384, F32), ("lw0", 96, U16), ("lw1", 48, U16),
-    ("sgn", 15 * 384, BF),
-    ("f0", 1536, BF), ("f1", 1280, BF), ("f2", 1024, BF), ("f3", 768, BF), ("f4", 512, BF), ("f5", 512, BF), ("f6", 768, BF),
-    ("dd0", 1536, BF), ("dd1", 768, BF), ("g30", 384, BF), ("g10", 384, BF), ("g31", 192, BF), ("g11", 192, BF),
-    ("lo", 512, BF), ("le", 512, BF), ("th0", 768, BF), ("ta1", 768, BF), ("tm", 512, BF), ("th1", 512, BF), ("ta3", 768, BF), ("tf", 1536, BF),
-    ("w1", 1536, BF), ("w0", 1536, BF), ("ty", 384, F32),
-    ("z1", 24, I32), ("z2", 24, F32), ("z3", 24, F32), ("c0", 24, U16), ("lpar", 12, F32), ("lown", 12, F32), ("lland", 12, I32),
-    ("lmix", 12, I32), ("yi", 24, I32), ("yf", 48, F32), ("c1", 12, U16),
+for _d, _l in [
+    (BF, "tx 1536 tua 512 tub 512 tv 512 t2 384 t4 96 ones 516 sgA 512 sgB 512 e0 516 en0 516 mM 384 mN 384 mN0 384 mR 384 m4 96 rb 384 "
+         "rs 3264 sgn 3456 f0 1536 f1 1280 f2 1024 f3 768 f4 512 f5 512 f6 768 dd0 1536 dd1 768 g30 384 g10 384 g31 192 g11 192 lo 512 le 512 "
+         "th0 768 ta1 768 tm 512 th1 512 dh0 768 dh1 384 ta3 768 tf 1536 w1 1536 w0 1536"),
+    (F32, "cf 8 cc 12 r16 24 jj 384 m2 384 kk 24 d1 384 px 384 rr0 24 rr1 12 sel 384 oo 576 sw 384 ty 384 yf 36"),
+    (I32, "ci 8 iw1 12 lland 12 yi 12"),
+    (U16, "pl 8 iu 36 lw0 96 lw1 48 c1 12"),
+    (Q4, "x 384 ua 128 ub 128 v 128 sa 128 sb 128 w2 512 e 512 en 512 sg 128 f 1408 lo0 128 l0 224 lo1 128 l1 176 h0 192 a1 192 hh 224 "
+         "st 272 a2 128 a3 192 fin 384"),
 ]:
-    SCRATCH[_n] = (S_, [128, _w], _d)
-for _n, _w in [("x", 384), ("ua", 128), ("ub", 128), ("v", 128), ("sa", 128), ("sb", 128), ("w2", 512), ("e", 512), ("en", 512), ("sg", 128),
-               ("f", 1408), ("lo0", 128), ("l0", 224), ("lo1", 128), ("l1", 176), ("h0", 192), ("h0n", 192), ("a1", 192), ("hh", 224),
-               ("st", 272), ("a2", 128), ("a3", 192), ("fin", 384)]:
-    SCRATCH["q" + _n] = (S_, [128, _w], Q4)
-    SCRATCH["s" + _n] = (S_, [128, _w], U8)
+    for _n, _w in zip(_l.split()[::2], _l.split()[1::2]):
+        if _d == Q4:
+            SCRATCH["q" + _n] = (S_, [128, int(_w)], Q4)
+            SCRATCH["s" + _n] = (S_, [128, int(_w)], U8)
+        else:
+            SCRATCH[_n] = (S_, [128, int(_w)], _d)
 
-SEMAPHORES = ["V", "S", "P", "G", "dx", "dx2", "dua", "dub", "dv", "dw", "sent", "a0", "a1", "am", "ah", "al", "a2", "oh"]
+SEMAPHORES = ["V", "S", "P", "G", "dx", "dx2", "dua", "dub", "dv", "dw", "sent", "a0", "a1", "am", "ah", "al", "a2", "oh", "dm"]
 
 
 def rank_program(g, core, T, topo):
@@ -47,11 +44,8 @@ def rank_program(g, core, T, topo):
     Q = {"V": g.vector, "S": g.scalar, "P": g.tensor, "G": g, "Y": g.sync}
     cnt = {n: 0 for n in SEMAPHORES}
     seen = {q: {} for q in Q}
-    lastw, readers = {}, {}
-    for n in SCRATCH:
-        w = SCRATCH[n][1][1]
-        lastw[n] = [None] * w
-        readers[n] = [None] * w
+    lastw = {n: [None] * SCRATCH[n][1][1] for n in SCRATCH}
+    readers = {n: [None] * SCRATCH[n][1][1] for n in SCRATCH}
 
     def v(n, a=0, b=None, s=1, ind=None):
         return (n, a, SCRATCH[n][1][1] if b is None else b, s, ind)
@@ -60,6 +54,8 @@ def rank_program(g, core, T, topo):
         return v("ps", 512 * k + a, 512 * k + b, s)
 
     def ap(x, cast=None):
+        if not isinstance(x, tuple):
+            return x
         n, a, b, s, ind = x
         r = T[n][:, a:b] if s == 1 else T[n][:, a:b:s]
         if cast is not None:
@@ -119,20 +115,14 @@ def rank_program(g, core, T, topo):
         call().then_inc(T.sem[q], 1)
         note((q, cnt[q]), reads, writes)
 
-    def arg(x):
-        return ap(x) if isinstance(x, tuple) else x
-
     def copy(o, i):
         run("V", lambda: g.vector.tensor_copy(ap(o), ap(i)), [i], [o])
 
     def tt(o, a, b, op):
         run("V", lambda: g.vector.tensor_tensor(ap(o), ap(a), ap(b), op), [a, b], [o])
 
-    def ts(o, a, s1, op0, s2=None, op1=None):
-        if op1 is None:
-            run("V", lambda: g.vector.tensor_scalar(ap(o), ap(a), arg(s1), None, op0), [a, s1], [o])
-        else:
-            run("V", lambda: g.vector.tensor_scalar(ap(o), ap(a), arg(s1), arg(s2), op0, op1), [a, s1, s2], [o])
+    def ts(o, a, s1, op0, s2=None, *op1):
+        run("V", lambda: g.vector.tensor_scalar(ap(o), ap(a), ap(s1), ap(s2), op0, *op1), [a, s1, s2], [o])
 
     def scan(o, a, b, op0, op1):
         run("V", lambda: g.vector.tensor_tensor_scan(ap(o), ap(a), ap(b), 0.0, op0, op1), [a, b], [o])
@@ -140,26 +130,22 @@ def rank_program(g, core, T, topo):
     def mset(o, c):
         run("V", lambda: g.vector.memset(ap(o), c), [], [o])
 
-    def act(o, i, fn, bias=None, scale=None, acc=None):
-        kw = {}
-        if bias is not None:
-            kw["bias"] = arg(bias)
-        if scale is not None:
-            kw["scale"] = arg(scale)
-        if acc is not None:
-            kw["accum_out"] = ap(acc)
-        run("S", lambda: g.scalar.activation(ap(o), ap(i), fn, **kw), [i, bias, scale], [o] + ([acc] if acc else []))
+    def act(o, i, fn, **kw):
+        acc = kw.get("accum_out")
+        run("S", lambda: g.scalar.activation(ap(o), ap(i), fn, **{k: ap(x) for k, x in kw.items()}),
+            [i, kw.get("bias"), kw.get("scale")], [o] + ([acc] if acc else []))
 
     def move(q, o, i, scale=None):
         if q == "S":
-            act(o, i, F.Copy, scale=scale)
+            act(o, i, F.Copy, **({} if scale is None else {"scale": scale}))
         elif scale is None:
             copy(o, i)
         else:
             ts(o, i, scale, A.mult)
 
     def quant(n, a, b, i):
-        run("V", lambda: g.vector.quantize_mx(ap(v("q" + n, a, b)), ap(v("s" + n, a, b)), ap(i)), [i], [v("q" + n, a, b), v("s" + n, a, b)])
+        o = [v("q" + n, a, b), v("s" + n, a, b)]
+        run("V", lambda: g.vector.quantize_mx(ap(o[0]), ap(o[1]), ap(i)), [i], o)
 
     def mm(k, w, wa, x, a, b, start=True, stop=True):
         r = [v("q" + w, wa, wa + 128), v("s" + w, wa, wa + 128), v("q" + x, a, b), v("s" + x, a, b)]
@@ -172,10 +158,8 @@ def rank_program(g, core, T, topo):
         act(v("s" + o, a, b), v("s" + src, ind=lst), F.Copy)
 
     def iota(o, pat, base=0, cm=0):
-        if SCRATCH[o[0]][2] == I32:
-            run("G", lambda: g.iota(ap(o), pat, base, cm), [], [o])
-        else:
-            run("G", lambda: g.iota(ap(o), pat, base, cm, allow_small_or_imprecise_dtypes=True), [], [o])
+        kw = {} if SCRATCH[o[0]][2] == I32 else {"allow_small_or_imprecise_dtypes": True}
+        run("G", lambda: g.iota(ap(o), pat, base, cm, **kw), [], [o])
 
     def asel(o, i, pat, op, base, cm):
         run("G", lambda: g.affine_select(ap(o), ap(i), pat, op, 0.0, base, cm), [i], [o])
@@ -184,11 +168,12 @@ def rank_program(g, core, T, topo):
         need(q, [], [o])
         cnt[sem] += 16
         Q[q].dma_start(ap(o, cast), src).then_inc(T.sem[sem], 16)
+        landed([o], sem)
 
-    def store(q, dst, src, i, sem):
+    def store(q, dst, src, i):
         need(q, [i], [])
-        cnt[sem] += 16
-        Q[q].dma_start(dst, src).then_inc(T.sem[sem], 16)
+        cnt["oh"] += 16
+        Q[q].dma_start(dst, src).then_inc(T.sem.oh, 16)
 
     def send(parts):
         need("G", [p[0] for p in parts], [])
@@ -224,302 +209,265 @@ def rank_program(g, core, T, topo):
     def cc(k):
         return v("cc", k, k + 1)
 
-    def unit(n, b):
-        a = 2 - (b & 2)
-        quant(n, 128 * b, 128 * b + 128, v("%s%d" % (n, b & 1), a, a + 512))
+    def ci(k):
+        return v("ci", k, k + 1)
 
     def pad(name, w, first):
         iota(v(name, 4 * first, 4 * w), [[0, 4 * (w - first)]])
 
     load("S", v("tua"), T.ua[:], "dua")
-    landed([v("tua")], "dua")
-    load("Y", v("tx", 0, 768), T.x[:, 0:768], "dx")
-    landed([v("tx", 0, 768)], "dx")
     load("Y", v("tx", 768, 1536), T.x[:, 768:1536], "dx2")
-    landed([v("tx", 768, 1536)], "dx2")
-    iota(v("ci", 0, 1), [[0, 1]], 0, 1)
-    iota(v("ci", 6, 7), [[0, 1]], 0, 2)
+    load("Y", v("tx", 0, 768), T.x[:, 0:768], "dx")
+    iota(ci(0), [[0, 1]], 0, 1)
     iota(v("r16"), [[16, 24]])
-    iota(v("t2"), [[0, 24], [2, 16]], -1)
+    iota(v("t2"), [[0, 24], [1, 16]])
     mset(v("ones"), 1.0)
-    mset(cc(3), BIG)
-    ts(v("ci", 2, 3), v("ci", 0, 1), 2, A.arith_shift_right, 3, A.bitwise_and)
-    ts(v("ci", 3, 4), v("ci", 0, 1), 3, A.bitwise_and)
-    ts(v("ci", 1, 2), v("ci", 6, 7), 31, A.bitwise_and)
+    asel(v("e0"), v("ones"), [[1, 516]], A.is_equal, -3, -4)
+    ts(ci(1), ci(0), 15, A.bitwise_and)
+    ts(ci(2), ci(0), 2, A.arith_shift_right, 3, A.bitwise_and)
+    ts(ci(3), ci(0), 1, A.bitwise_and)
+    for u in (3, 4, 5):
+        mset(v("f%d" % u, 4 * FIRST[u]), 0.0)
     copy(v("pl"), v("r16", 0, 8))
     copy(v("cf", 1, 4), v("ci", 1, 4))
-    act(v("rr0"), v("r16"), F.Copy, scale=0.0)
-    act(v("rr1"), v("r16", 0, 12), F.Copy, scale=0.0)
-    ts(cc(1), cf(1), (B - 1) / 2, A.mult, 15 * (1 - B), A.add)
-    ts(cc(8), cf(2), -4 * B, A.mult, 12 * B, A.add)
-    ts(v("mM"), v("t2"), cf(1), A.subtract, BIG, A.mult)
-    act(v("mN0"), v("mM"), F.Abs, bias=cc(3))
-    for u in (0, 2, 3):
-        pad("f%d" % u, FW[u], FW[u] - 48)
-    iota(v("t4"), [[0, 24], [1, 4]])
-    pad("f1", FW[1], FW[1] - 48)
-    pad("f4", 128, 80)
-    pad("f5", 128, 16)
+    act(cc(1), cf(1), F.Identity, scale=B - 1, bias=15 - 17 * B)
+    act(cc(4), cf(1), F.Identity, scale=-1.0, bias=0.5)
+    act(v("kk"), v("r16"), F.Identity, bias=cc(1))
+    ts(v("mN"), v("t2"), cf(1), A.not_equal, -BIG, A.mult)
+    quant("ua", 0, 128, v("tua"))
+    ts(v("mM"), v("t2"), -0.5, A.add, BIG, A.mult)
+    pick("sa", 0, 128, "ua", v("pl"))
+    act(v("mN0"), v("t2"), F.Sign, bias=cc(4))
+    act(v("m2"), v("mN0"), F.Identity, scale=B)
+    for u in (1, 0, 2):
+        pad("f%d" % u, FW[u], FIRST[u])
     asel(v("sgA"), v("ones", 0, 512), [[-16, 8], [0, 64]], A.is_ge, 0, 1)
     asel(v("sgB"), v("sgA"), [[16, 8], [0, 64]], A.is_ge, 15, -1)
-    for u in range(2):
-        asel(v("e%d" % u), v("ones"), [[1, 514]], A.is_equal, -2 - u, -4)
     iota(v("jj"), [[1, 384]])
     pad("lo", 128, 96)
-    iota(v("le", 0, 128), [[0, 128]])
+    pad("le", 32, 0)
     pad("f6", 192, 144)
-    iota(v("th1", 0, 128), [[0, 128]])
-    iota(v("tm", 0, 320), [[0, 320]])
-
-    quant("ua", 0, 128, v("tua"))
-    ts(v("kk"), v("r16"), cc(1), A.add)
-    pick("sa", 0, 128, "ua", v("pl"))
-    act(v("mN"), v("mN0"), F.Identity, bias=cc(3), scale=-1.0)
-    quant("x", 0, 192, v("tx", 0, 768))
+    pad("th1", 32, 0)
+    pad("tm", 80, 0)
     quant("x", 192, C, v("tx", 768, 1536))
-    ts(v("mR"), v("t2"), 0.0, A.is_gt)
-    ts(v("m2"), v("mM"), -16 * B, A.max, B, A.min)
+    mm(3, "sa", 0, "x", 256, C)
+    quant("x", 0, 192, v("tx", 0, 768))
     need("Y", [v("tx")], [])
     load("Y", v("qw2"), T.wc[:], "dw", dt.uint8)
     load("Y", v("sw2"), T.ws[:], "dw")
-    landed([v("qw2"), v("sw2")], "dw")
+    landed([v("qw2")], "dw")
     load("Y", v("tub"), T.ub[:], "dub")
-    landed([v("tub")], "dub")
     load("Y", v("tv"), T.v[:], "dv")
-    landed([v("tv")], "dv")
-
-    fill = []
-
-    def idle(k):
-        for _ in range(min(k, len(fill))):
-            fill.pop(0)()
 
     def down(l, s, a):
         n = C >> l
-        nb, ns, h = n // 16, NS[l], n // 4
-        nv = nb - 1 - ns
+        nb, h = n // 16, n // 4
         tiles = ["f0", "f1", "f2", "f3", "f4", "f5"] if l == 0 else ["f6", "f4", "f5"]
-        wid = [SCRATCH[t][1][1] // 4 for t in tiles]
+        wid = FW if l == 0 else FW[3:]
         off = [sum(wid[:u]) for u in range(len(wid))]
-        oo, rr, sa = C * l, "rr%d" % l, SA[l]
-        iw, lw, dd, g3 = "iw%d" % l, "lw%d" % l, "dd%d" % l, "g3%d" % l
+        oo, rr, iu = C * l, "rr%d" % l, v("iu", 24 * l, 24 * l + nb)
+        lw, dd, g3 = "lw%d" % l, "dd%d" % l, "g3%d" % l
+        sr, ks = SR[l], min(SR[l])
 
-        def slot(r, w):
+        def slot(r, w, first=0):
             k = nb - r
-            return v(tiles[k // 4], k % 4, 4 * w, 4)
+            return v(tiles[k // 4], 4 * first + k % 4, 4 * w, 4)
+
+        def xx(a_, b_):
+            return v("m2", 16 * a_ + 15, 16 * b_, 16)
 
         def own(r):
             return v("px", 16 * r + 15, 16 * r + 16)
-
-        def unpack(b):
-            if l == 0:
-                unit("e", b)
-            mm(4 + b, "e", 128 * b, a, 0, n)
-
-        def halve(b):
-            act(v(dd, b, 4 * n, 4), bank(4 + b, 0, n), F.Copy, scale=0.5)
-
-        def evens():
-            lists(l, 2)
-            move("S", v("g1%d" % l), v(dd, ind=v(lw, 2 * nb, 3 * nb)))
         mm(1, s, 0, a, 0, n)
         mm(0, s, 0, a, 0, n)
         if l == 1:
             for b in range(4):
-                unpack(b)
-        idle(2)
-        top = 16 * (nb - TOP[l])
-        tt(v("d1", top, n), bank(1, top, n), v("mN", top, n), A.min)
-        if l == 0:
-            ts(cc(2), cc(8), cf(3), A.add)
-        scan(v("px", top, n), v("mM", top, n), v("d1", top, n), A.min, A.max)
-        tt(v("d1", 0, top), bank(0, 0, top), v("mN", 0, top), A.min)
-        if l == 0:
-            ts(v("m4"), v("t4"), cf(2), A.is_le, 5 * B, A.mult)
-        scan(v("px", 0, top), v("mM", 0, top), v("d1", 0, top), A.min, A.max)
-        for k in range(ns + 1):
-            if k < ns:
-                r = nb - 1 - k
-                act(v("sgn", 384 * k, 384 * k + 16 * r), bank(1, 0, 16 * r), F.Sign, bias=own(r), scale=-1.0)
-            if k > 0:
-                r = nb - k
-                act(slot(r, 16 * r), v("sgn", 384 * (k - 1), 384 * (k - 1) + 16 * r), F.Relu, acc=v(rr, r, r + 1))
-        done = []
-
-        def sums(u):
-            if l == 0 and not done:
+                mm(4 + b, "e", 128 * b, a, 0, n)
+        done, z = [], (n, n)
+        for x in VR[l]:
+            if isinstance(x, int):
+                ts(slot(x, 16 * x), bank(0, 0, 16 * x), own(x), A.is_lt)
+            elif x[0] == "o":
+                z = (int(x[1:]), z[0])
+                tt(v("d1", *z), bank(3, 64, 128) if z[0] == 320 else bank(1 if z[0] else 0, *z), v("mN", *z), A.add)
+            elif x == "s":
+                scan(v("px", *z), v("mM", *z), v("d1", *z), A.min, A.max)
+            elif x == "S":
+                for k in range(len(sr) + 1):
+                    if k < len(sr):
+                        r = sr[k]
+                        act(v("sgn", 384 * k, 384 * k + 16 * r), bank(1, 0, 16 * r), F.Sign, bias=own(r), scale=-1.0)
+                    if k > 0:
+                        r = sr[k - 1]
+                        act(slot(r, 16 * r), v("sgn", 384 * (k - 1), 384 * (k - 1) + 16 * r), F.Relu, accum_out=v(rr, r, r + 1))
+            elif x == "R":
+                ts(v("mR"), v("t2"), 1.0, A.min)
+            elif x == "g":
                 quant("sg", 0, 128, v("sgB"))
-            quant("f", off[u], off[u] + wid[u], v(tiles[u]))
-            mm(2, "sg", 0, "f", off[u], off[u] + wid[u], not done, len(done) == len(tiles) - 1)
-            done.append(u)
-        extra = {nv: lambda: tt(slot(nb, n), bank(0, 0, n), v("px", 0, n), A.is_le),
-                 nv - 1: lambda: scan(v("rb", 0, n), v("mR", 0, n), slot(nb, n), A.mult, A.add),
-                 nv - 2: lambda: tt(v("xx", 0, nb), v("kk", 0, nb), v("rb", 15, n, 16), A.subtract)}
-        for r in range(nv, -1, -1):
-            if r > 0:
-                ts(slot(r, 16 * r), bank(0, 0, 16 * r), own(r), A.is_lt)
-            if 0 < r <= sa:
-                act(v("sgn", 3456 + 160 * r, 3456 + 176 * r), slot(r, 16 * r), F.Identity, acc=v(rr, r, r + 1))
-            if sa <= r < nv:
-                scan(v("rs", 240 * r + 240, 256 * r + 256), v("ones", 0, 16 * r + 16), slot(r + 1, 16 * r + 16), A.mult, A.add)
-            if r in extra:
-                extra[r]()
-            if r == 3:
-                idle(2)
-            for u in WHEN[l].get(r, ()):
-                sums(u)
-        if sa < nv:
-            tt(v("xx", sa + 1, nv + 1), v("xx", sa + 1, nv + 1), v("rs", 256 * sa + 255, 256 * nv, 256), A.subtract)
-        idle(3)
+            elif x == "i":
+                quant("v", 0, 128, v("tv"))
+            elif x[0] == "e":
+                b = int(x[1])
+                quant("e", 128 * b, 128 * b + 128, v("e0", 3 - b, 515 - b))
+                mm(4 + b, "e", 128 * b, a, 0, n)
+            elif x == "d":
+                tt(slot(nb, n), bank(0, 0, n), v("px", 0, n), A.is_le)
+            elif x == "b":
+                scan(v("rb", 0, n), v("mR", 0, n), slot(nb, n), A.mult, A.add)
+            elif x == "k":
+                tt(xx(0, nb), v("kk", 0, nb), v("rb", 15, n, 16), A.subtract)
+            elif x == "w":
+                tt(xx(ks, nb), xx(ks, nb), v(rr, ks, nb), A.subtract)
+            elif x == "v":
+                tt(xx(1, ks), xx(1, ks), v("rs", 383, 192 * ks, 192), A.subtract)
+            elif x[0] == "r":
+                r = int(x[1:])
+                scan(v("rs", 184 * r + 192, 192 * r + 192), slot(r, 8 * r), slot(r, 16 * r, 8 * r), A.add, A.add)
+            else:
+                u = int(x[1:])
+                quant("f", off[u], off[u] + wid[u], v(tiles[u]))
+                mm(2, "sg", 0, "f", off[u], off[u] + wid[u], not done, len(done) == len(tiles) - 1)
+                done.append(u)
         if l == 0:
-            unpack(0)
-            unpack(2)
-        for b in (0, 2) if l == 0 else range(4):
-            halve(b)
-        scan(v("sel", 0, n), v("m2", 0, n), bank(2, 0, n), A.add, A.max)
-        tt(v("xx", 0, nb), v("xx", 0, nb), v(rr), A.subtract)
-        if l == 0:
-            unpack(1)
-            halve(1)
-        idle(1)
-        tt(v(iw), v("sel", 15, n, 16), v("xx", 0, nb), A.add)
-        if l == 0:
-            unpack(3)
-            halve(3)
-        idle(1)
-        copy(v("iu", 0, nb), v(iw))
-        idle(1)
-        if l == 0:
-            ts(v("m4"), v("m4"), -B, A.add)
+            act(cc(9), cf(2), F.Identity, scale=4.0, bias=2.0)
+            act(cc(8), cf(2), F.Identity, scale=-4 * B - 4, bias=12 * B)
+            act(v("t4"), v("t2", 0, 384, 4), F.Sign, bias=cc(9), scale=-1.0)
+            act(cc(2), cc(8), F.Identity, bias=cf(1))
+            act(v("m4"), v("t4"), F.Identity, bias=1.5 * B, scale=2.5 * B)
+        for b in (0, 2, 1, 3):
+            act(v(dd, b, 4 * n, 4), bank(4 + b, 0, n), F.Copy, scale=0.5)
+        scan(v("sel", 0, n), bank(2, 0, n), v("m2", 0, n), A.max, A.add)
+        ts(iu, v("sel", 15, n, 16), 2 * B, A.add)
         if l == 1:
+            ts(v("iw1"), v("sel", 15, n, 16), 2 * B, A.add)
             send([(v("iw1"), v("lland"), rank ^ 1, "al")])
             landed([v("lland")], "al")
-        copy(v("oo", oo, oo + n, ind=v("iu", 0, nb)), v("jj", 0, n))
+        copy(v("oo", oo, oo + n, ind=iu), v("jj", 0, n))
+        scans(l, 0)
         lists(l, 0)
+        move("S", v(g3, n // 2, n), v(dd, ind=v(lw, nb // 2, nb)))
+        move("V", v(g3, 0, n // 2), v(dd, ind=v(lw, 0, nb // 2)))
         if l == 0:
-            move("S", v(g3, n // 2, n), v(dd, ind=v(lw, nb // 2, nb)))
-            move("V", v(g3, 0, n // 2), v(dd, ind=v(lw, 0, nb // 2)))
+            quant("ub", 0, 128, v("tub"))
         else:
-            move("S", v(g3), v(dd, ind=v(lw, 0, nb)))
-            evens()
-        tt(v("lo", 0, n), v(dd, ind=v(lw, nb, 2 * nb)), v(g3), A.add)
+            scans(l, 2)
+        tt(v("lo", 0, n // 2), v(dd, ind=v(lw, nb, 3 * nb // 2)), v(g3, 0, n // 2), A.add)
+        if l == 1:
+            lists(l, 2)
+            move("S", v("g11"), v(dd, ind=v(lw, 2 * nb, 3 * nb)))
+        tt(v("lo", n // 2, n), v(dd, ind=v(lw, 3 * nb // 2, 2 * nb)), v(g3, n // 2, n), A.add)
         quant("lo%d" % l, 0, 128, v("lo"))
         cross("lo%d" % l, 0, h, [("l%d" % l, 128, rank ^ (1 << l))], "a%d" % l)
-        if l == 0:
-            evens()
+
+    def scans(l, k0):
+        n = C >> l
+        for k in (k0, k0 + 1):
+            scan(v("sw", k * n // 4, (k + 1) * n // 4), v("m4", 0, n // 4), v("oo", C * l + 3 - k, C * l + n, 4), A.add, A.min)
 
     def lists(l, k0):
-        n = C >> l
-        h, nb, oo = n // 4, n // 16, C * l
-        for k in (k0, k0 + 1):
-            scan(v("sw", k * h, (k + 1) * h), v("m4", 0, h), v("oo", oo + 3 - k, oo + n, 4), A.add, A.min)
+        h, nb = 96 >> l, 24 >> l
         ts(v("lw%d" % l, k0 * nb, (k0 + 2) * nb), v("sw", k0 * h + 3, (k0 + 2) * h, 4), 4.0, A.mult, cc(2), A.add)
 
-    def layer(x, a, k0, h, out, who="VSVS"):
+    def layer(x, a, k0, h, out):
         for b in range(4):
             mm(k0 + b, "w2", 128 * b, x, a, a + 128)
         for b in range(4):
-            move(who[b], out(b), bank(k0 + b, 128 - h, 128), 0.03125)
+            move("V", out(b), bank(k0 + b, 128 - h, 128), 0.03125)
 
     down(0, "sa", "x")
-    tt(v("th0", 0, 384), v("dd0", ind=v("lw0", 24, 48)), v("g30"), A.subtract)
-    quant("ub", 0, 128, v("tub"))
-    tt(v("le", 128, 512), v("dd0", ind=v("lw0", 72, 96)), v("g10"), A.add)
+    scans(0, 2)
+    lists(0, 2)
+    move("S", v("g10", 192, 384), v("dd0", ind=v("lw0", 60, 72)))
+    move("V", v("g10", 0, 192), v("dd0", ind=v("lw0", 48, 60)))
     pick("sb", 0, 128, "ub", v("pl"))
-    for u in range(2):
-        act(v("en%d" % u), v("e%d" % u), F.Copy, scale=-1.0)
+    act(cc(6), cf(3), F.Copy, scale=192.0)
+    act(v("en0"), v("e0"), F.Copy, scale=-1.0)
+    tt(v("le", 128, 512), v("dd0", ind=v("lw0", 72, 96)), v("g10"), A.add)
     quant("l0", 0, 128, v("le"))
-    ts(v("ci", 4, 5), v("ci", 0, 1), 1, A.bitwise_and)
-    ts(v("ci", 5, 6), v("ci", 0, 1), 1, A.arith_shift_right, 7, A.bitwise_and)
-    layer("l0", 0, 0, 96, lambda b: v("ta1", b, 768, 8), "SSSS")
-    copy(v("cf", 4, 6), v("ci", 4, 6))
-    unit("en", 0)
-    unit("en", 2)
+    layer("l0", 0, 0, 96, lambda b: v("ta1", b, 768, 8))
     layer("l0", 96, 4, 96, lambda b: v("ta1", 4 + b, 768, 8))
     quant("a1", 0, 192, v("ta1"))
-    fill.extend([lambda: unit("en", 1), lambda: unit("en", 3),
-                 lambda: ts(v("z1"), v("iw0"), 1, A.bitwise_and),
-                 lambda: ts(cc(5), cf(4), -1.0, A.mult, 1.0, A.add),
-                 lambda: ts(v("z2"), v("z1"), 383.0, A.mult),
-                 lambda: ts(cc(7), cc(5), 96.0, A.mult, cf(5), A.add),
-                 lambda: tt(v("z3"), v("z2"), v("iw0"), A.add),
-                 lambda: ts(cc(6), cf(4), 96.0, A.mult),
-                 lambda: ts(v("hl"), v("r16", 0, 12), 0.5, A.mult, cc(7), A.add),
-                 lambda: ts(v("c0"), v("z3"), 0.5, A.mult)])
 
     down(1, "sb", "a1")
-    idle(len(fill))
-    store("Y", T.ol[:], T.oo[0:128:16, :], v("oo"), "oh")
-    tt(v("le", 320, 512), v("dd1", ind=v("lw1", 36, 48)), v("g11"), A.add)
+    store("Y", T.ol[:], T.oo[0:128:16, :], v("oo"))
+    need("Y", [v("iw1")], [v("lland")])
+    cnt["dm"] += 16
+    g.sync.dma_start(T.lland[0:128:2, :], T.iw1[0:128:2, :]).then_inc(T.sem.dm, 16)
+    landed([v("lland")], "dm")
     tt(v("th1", 320, 512), v("dd1", ind=v("lw1", 12, 24)), v("g31"), A.subtract)
-    quant("l1", 0, 128, v("le"))
+    tt(v("le", 320, 512), v("dd1", ind=v("lw1", 36, 48)), v("g11"), A.add)
     tt(v("th1", 128, 320), v("dd1", ind=v("lw1", 36, 48)), v("g11"), A.subtract)
+    quant("l1", 0, 128, v("le"))
     for b in range(4):
         mm(b, "w2", 128 * b, "l1", 0, 128)
     quant("hh", 0, 128, v("th1"))
     cross("hh", 32, 96, [("hh", 128, rank ^ 1)], "ah")
     for b in range(4):
-        move("SSVS"[b], v("tm", 320 + b, 512, 4), bank(b, 80, 128), 0.03125)
+        move("V", v("tm", 320 + b, 512, 4), bank(b, 80, 128), 0.03125)
     quant("st", 0, 128, v("tm"))
     cross("st", 80, 48, [("st", 176, rank ^ 1)], "am")
     layer("l1", 48, 4, 48, lambda b: v("lo", b, 192, 4))
     quant("a2", 0, 128, v("lo"))
     cross("a2", 0, 48, [("st", 128, rank ^ 2), ("st", 224, rank ^ 3)], "a2")
 
-    order = [(0, 0), (2, 0), (0, 1), (2, 1), (1, 0), (3, 0), (1, 1), (3, 1)]
-    sign = ("e", "en")
-    for k, (b, s) in enumerate(order):
-        mm(k, sign[s], 128 * b, "hh", 32, 224, True, False)
+    def pair(w, d, b, k):
+        for s, op in enumerate((A.add, A.subtract)):
+            tt(v(w, 384 * b + s, 384 * b + 384, 2), bank(k, 0, 192), v(d, 192 * b, 192 * b + 192), op)
+    for b in (2, 3):
+        quant("en", 128 * b, 128 * b + 128, v("en0", 3 - b, 515 - b))
+    for b in range(2):
+        mm(b, "e", 128 * b, "hh", 32, 224)
+    for k in range(4):
+        mm(4 + k, ("e", "en")[k & 1], 256 + 128 * (k // 2), "hh", 32, 224, True, False)
+    for b in range(2):
+        move("S", v("dh1", 192 * b, 192 * b + 192), bank(b, 0, 192))
+    tt(v("th0", 0, 384), v("dd0", ind=v("lw0", 24, 48)), v("g30"), A.subtract)
+    ts(v("yi"), v("lland"), 3, A.bitwise_and)
     tt(v("th0", 384, 768), v("dd0", ind=v("lw0", 72, 96)), v("g10"), A.subtract)
-    ts(v("lpar"), v("lland"), cf(4), A.mult)
-    ts(v("lown"), v("iw1"), cc(5), A.mult)
+    ts(v("yf", 0, 12), v("yi"), 2.0, A.is_ge, 188.0, A.mult)
+    tt(v("yf", 12, 24), v("yi"), v("lland"), A.add)
     quant("h0", 0, 192, v("th0"))
-    tt(v("lmix"), v("lown"), v("lpar"), A.add)
-    pick("h0n", 0, 192, "h0", v("hl"))
-    ts(v("yi", 0, 12), v("lmix"), 1, A.bitwise_and)
-    ts(v("yi", 12, 24), v("lmix"), 2, A.bitwise_and)
-    ts(v("yf", 0, 12), v("yi", 0, 12), 767.0, A.mult)
-    ts(v("yf", 24, 36), v("yi", 12, 24), 95.0, A.mult)
-    tt(v("yf", 12, 24), v("yf", 0, 12), v("lmix"), A.add)
-    quant("v", 0, 128, v("tv"))
-    tt(v("yf", 36, 48), v("yf", 12, 24), v("yf", 24, 36), A.add)
-    ts(v("c1"), v("yf", 36, 48), 0.25, A.mult, cc(6), A.add)
-    for k, (b, s) in enumerate(order):
-        mm(k, "e", 128 * b, "st", 80, 272, False, True)
-    for k, (b, s) in enumerate(order):
-        move("VS"[b // 2], v("w1", 384 * b + 192 * s, 384 * b + 192 * s + 192), bank(k, 0, 192))
-    for b in (0, 2, 1, 3):
-        move("VS"[b // 2], v("ta3", b, 768, 4), v("w1", 384 * b, 384 * b + 384, ind=v("c1")))
-    for k, (b, s) in enumerate(order):
-        mm(k, sign[s], 128 * b, "h0n", 0, 192, True, False)
+    tt(v("yf", 24, 36), v("yf", 0, 12), v("yf", 12, 24), A.add)
+    ts(v("c1"), v("yf", 24, 36), 0.5, A.mult, cc(6), A.add)
+    for k in (0, 4, 5, 1, 6, 7):
+        mm(k, "e", 128 * k if k < 4 else 128 * (k // 2), "st", 80, 272, k < 4, True)
+    for b in (2, 3):
+        mm(b, "e", 128 * b, "h0", 0, 192)
+    pair("w1", "dh1", 0, 0)
+    pair("w1", "dh1", 1, 1)
+    for k in range(4):
+        move("S", v("w1", 768 + 384 * (k // 2) + k % 2, 1152 + 384 * (k // 2), 2), bank(4 + k, 0, 192))
+    for b in (0, 2, 1):
+        move("VVS"[b], v("ta3", b, 768, 4), v("w1", 384 * b, 384 * b + 384, ind=v("c1")))
+    move("S", v("ta3", 3, 384, 4), v("w1", 1152, 1536, ind=v("c1", 0, 6)))
+    move("V", v("ta3", 387, 768, 4), v("w1", 1152, 1536, ind=v("c1", 6, 12)))
+    for b in (0, 1):
+        mm(4 + b, "e", 128 * b, "h0", 0, 192)
+    for b, k in ((0, 4), (1, 5), (2, 2), (3, 3)):
+        move("S", v("dh0", 192 * b + 1, 192 * b + 192, 2), bank(k, 0, 96))
+        move("S", v("dh0", 192 * b, 192 * b + 192, 2), bank(k, 96, 192))
     quant("a3", 0, 192, v("ta3"))
 
-    for k, (b, s) in enumerate(order):
-        mm(k, "e", 128 * b, "a3", 0, 192, False, True)
-    for k, (b, s) in enumerate(order):
-        move("VS"[b // 2], v("w0", 384 * b + 192 * s, 384 * b + 192 * s + 192), bank(k, 0, 192))
-
-    def back(b, a, e):
-        move("VS"[b // 2], v("tf", 4 * a + b, 4 * e, 4), v("w0", 384 * b, 384 * b + 384, ind=v("c0", a // 16, e // 16)))
-
-    def finish(k, a, e):
-        quant("fin", a, e, v("tf", 4 * a, 4 * e))
-        mm(k, "v", 0, "fin", a, e)
-        store("Y", T.oc[:, 4 * a:4 * e], T.qfin[:, a:e].bitcast(dt.uint8), v("qfin", a, e), "oh")
-    for b in (0, 2, 1, 3):
-        back(b, 0, CUT)
-    back(2, CUT, C)
-    finish(0, 0, CUT)
-    back(0, CUT, C)
-    back(3, CUT, C)
-    back(1, CUT, C)
-    move("S", v("ty", 0, CUT), bank(0, 0, CUT))
-    finish(1, CUT, C)
-    move("V", v("ty", CUT, C), bank(1, 0, C - CUT))
-    store("S", T.y[:, 0:CUT], T.ty[:, 0:CUT], v("ty", 0, CUT), "oh")
+    for b in range(4):
+        mm((0, 1, 6, 7)[b], "e", 128 * b, "a3", 0, 192)
+    for b in range(4):
+        pair("w0", "dh0", b, (0, 1, 6, 7)[b])
+    for x in TAIL:
+        a, e = ((0, CUT), (CUT, C))[x[-1] == "1"]
+        if x[0] == "f":
+            quant("fin", a, e, v("tf", 4 * a, 4 * e))
+            mm(4 + int(x[1]), "v", 0, "fin", a, e)
+            store("Y", T.oc[:, 4 * a:4 * e], T.qfin[:, a:e].bitcast(dt.uint8), v("qfin", a, e))
+        elif x == "y":
+            move("S", v("ty", 0, CUT), bank(4, 0, CUT))
+        else:
+            b = int(x[1])
+            move(x[0], v("tf", 4 * a + b, 4 * e, 4), v("w0", 384 * b, 384 * b + 384, ind=v("iu", a // 16, e // 16)))
+    move("V", v("ty", CUT, C), bank(5, 0, C - CUT))
+    store("S", T.y[:, 0:CUT], T.ty[:, 0:CUT], v("ty", 0, CUT))
     for k in range(4):
-        store("Y", T.osc[4 * k:4 * k + 4, :], T.sfin[32 * k:32 * k + 4, :], v("sfin"), "oh")
-    store("S", T.y[:, CUT:C], T.ty[:, CUT:C], v("ty", CUT, C), "oh")
+        store("Y", T.osc[4 * k:4 * k + 4, :], T.sfin[32 * k:32 * k + 4, :], v("sfin"))
+    store("S", T.y[:, CUT:C], T.ty[:, CUT:C], v("ty", CUT, C))
     for n in SEMAPHORES:
         if cnt[n] and seen["G"].get(n, 0) < cnt[n]:
             g.wait_ge(T.sem[n], cnt[n])

@@ -1,31 +1,47 @@
 from concourse.bass import DstId, RemoteDMATransfer
 from concourse.mybir import dt, AluOpType as A, ActivationFunctionType as F
 
+SLOTS = (tuple(range(24, 0, -1)), (12, 8, 7, 6, 11, 10, 9, 5, 4, 3, 2, 1))
+LATE = (160, 192)
 C = 384
+ORDER = tuple(int(_k) for _k in """
+5 3 0 1 2 4 7 10 11 12 13 17 25 26 14 27 28 47 40 19 23 22 20 21 29 24 41 18 42 53 6 8 43 44 45 48 57 49 55 66 54 149 71 58 59 46 50 51 52 56
+16 9 30 32 15 31 33 34 35 36 75 63 65 60 72 61 73 64 62 94 79 81 91 82 85 76 77 74 84 83 78 123 99 121 120 95 124 96 80 128 112 130 101 89 122
+114 92 131 129 100 90 93 102 113 104 108 109 97 103 98 117 107 127 132 126 125 88 87 86 139 137 70 69 67 106 105 110 111 116 115 118 119 133
+138 68 134 140 150 135 141 136 142 154 147 146 144 145 143 156 157 158 160 163 153 162 159 165 161 166 168 151 170 167 171 148 37 38 39 164 169
+173 175 179 177 181 176 178 180 182 152 155 172 185 184 189 186 190 188 183 187 191 192 199 193 195 196 197 194 200 201 213 216 210 209 215 214
+202 204 203 205 207 206 219 211 229 208 232 230 231 212 225 217 220 226 223 224 222 228 234 240 241 238 239 233 218 221 227 235 236 237 245 244
+246 247 249 248 259 260 252 250 251 253 254 255 257 256 263 261 262 269 258 265 267 266 264 271 272 268 270 278 279 281 280 273 174 275 282 283
+285 284 288 292 276 299 274 277 198 286 287 304 293 294 296 307 289 305 306 242 300 309 290 310 295 301 243 312 311 308 291 313 315 318 319 325
+317 314 324 331 322 323 316 320 321 330 332 333 297 298 302 326 328 303 327 329 334 335 340 336 338 341 343 342 346 337 339 345 344 347 349 350
+348 351 358 353 354 356 352 355 357 361 363 364 359 360 362 365 366
+""".split())
 BIG = float(2 ** 80)
 B = 1024.0
-SR = ((23, 22, 21, 20, 19, 18, 17), (11, 10, 9))
-VR = (("e0", "e2", "o320", "e1", "s", "e3", "o0", "R", "s", "S", 16, "d", 15, 14, "r16", "b", 13, "r15", 12, "r14", "k", 11, "r13", 10, "r12",
-       9, "r11", "g", "q0", 8, "r10", 7, "r9", 6, "r8", 5, "r7", "q3", 4, "r6", 3, "r5", "q4", 2, "r4", 1, "r3", "q2", "q1", "r2", "q5", "r1",
-       "w", "v"),
-      ("i", "o128", "s", "o0", "s", "S", 8, "d", 7, 6, "r8", "b", 5, "r7", 4, "r6", "k", 3, "r5", 2, "r4", 1, "q0", "q1", "r3", "r2", "q2",
-       "r1", "w", "v"))
-TAIL = ("S00", "S10", "S20", "V30", "V01", "f0", "S11", "S21", "V31", "y", "f1")
-CUT = 256
+VR = (("u", "X", "e0", "N", "e2", "x", "M", "o320", "m1", "m0", "e1", "e3", "s", "A23", "A22", "B23", "A21", "B22", "A20", "o192", "E", "s",
+       "B21", "A19", "B20", "A18", "B19", "B18", 17, "o0", 16, 15, "s", "A8", "A7", "A6", "B8", "B7", "B6", 14, "r17", 13, "d", "r16", 12,
+       "r15", 11, "r14", "b", 10, "r13", 9, "g", "r12", "q0", "k", "r11", "q2", "r10", "r9", "q3", "q1", 5, 4, 3, 2, 1, "w17-24", "v9-17",
+       "r5", "r4", "r3", "r2", "r1", "q5", "p1", "q4", "v1-6", "w6-9", "p0"),
+      ("m1", "m0", "E", "H", "n", "o0", "s", "A11", "A10", "A9", "B11", "B10", "B9", 8, 7, "d", 6, 5, 4, 3, 2, 1, "q0", "b", "q2", "r8", "r7",
+       "k", "r6", "q1", "r5", "r4", "r3", "r2", "r1", "v1-9", "w9-12", "p0"))
+UP1 = ("S30", "S00", "V20", "V10")
+TAIL = ("V10", "S00", "S30", "V20", "S01", "f0", "S31", "V21", "V11", "yS0", "f1", "yV1")
+CUTS = (0, 256, 384)
 FW = (384, 320, 256, 192, 128, 128)
 FIRST = (336, 272, 208, 144, 80, 16)
+SPLIT = (128, 96)
 
 S_, BF, F32, I32, U16, Q4, U8 = "sbuf", "bfloat16", "float32", "int32", "uint16", "float8_e4m3fn_x4", "uint8"
 SCRATCH = {"ps": ("psum", [128, 4096], F32)}
 for _d, _l in [
-    (BF, "tx 1536 tua 512 tub 512 tv 512 t2 384 t4 96 ones 516 sgA 512 sgB 512 e0 516 en0 516 mM 384 mN 384 mN0 384 mR 384 m4 96 rb 384 "
-         "rs 3264 sgn 3456 f0 1536 f1 1280 f2 1024 f3 768 f4 512 f5 512 f6 768 dd0 1536 dd1 768 g30 384 g10 384 g31 192 g11 192 lo 512 le 512 "
-         "th0 768 ta1 768 tm 512 th1 512 dh0 768 dh1 384 ta3 768 tf 1536 w1 1536 w0 1536"),
-    (F32, "cf 8 cc 12 r16 24 jj 384 m2 384 kk 24 d1 384 px 384 rr0 24 rr1 12 sel 384 oo 576 sw 384 ty 384 yf 36"),
-    (I32, "ci 8 iw1 12 lland 12 yi 12"),
-    (U16, "pl 8 iu 36 lw0 96 lw1 48 c1 12"),
-    (Q4, "x 384 ua 128 ub 128 v 128 sa 128 sb 128 w2 512 e 512 en 512 sg 128 f 1408 lo0 128 l0 224 lo1 128 l1 176 h0 192 a1 192 hh 224 "
-         "st 272 a2 128 a3 192 fin 384"),
+    (BF, "tx 1536 tua 512 tub 512 tv 512 t2 384 t4 96 ones 516 sgA 512 sgB 512 e0 516 en0 512 mM 192 mN 192 m4 96 rb 384 "
+         "rs 3264 sgn 4416 f0 1536 f1 1280 f2 1024 f3 768 f4 512 f5 512 f6 768 f7 704 dd0 1536 dd1 768 g30 384 g10 384 g31 192 g11 192 lo 512 "
+         "la 512 le 512 th0 768 ta1 768 tm 512 th1 512 dh0 576 dh1 576 ta3 768 tf 1536 w1 1536 w0 1536"),
+    (F32, "cf 8 cc 12 r16 24 jj 384 m2 384 kk 24 d1 384 px 384 rr 168 sel 384 oo 576 sw 384 ty 384 yf 36"),
+    (I32, "ci 8 yw 12 yi 12"),
+    (U16, "pl 8 iu 36 lw0 96 lw1 48 c1 12 lland 12 nat 12"),
+    (Q4, "x 384 ua 128 ub 128 v 128 sa 128 sb 128 w2 512 e 512 en 128 sg 128 f 1408 lo0 256 l0 224 lo1 128 l1 176 h0 192 hn 192 "
+         "a1 192 hh 224 st 272 a2 128 a3 192 fin 384"),
 ]:
     for _n, _w in zip(_l.split()[::2], _l.split()[1::2]):
         if _d == Q4:
@@ -34,7 +50,7 @@ for _d, _l in [
         else:
             SCRATCH[_n] = (S_, [128, int(_w)], _d)
 
-SEMAPHORES = ["V", "S", "P", "G", "dx", "dx2", "dua", "dub", "dv", "dw", "sent", "a0", "a1", "am", "ah", "al", "a2", "oh", "dm"]
+SEMAPHORES = ["V", "S", "P", "G", "dx", "dx2", "dua", "dub", "dv", "dw", "sent", "a0", "a9", "a1", "am", "ah", "al", "a2", "oh", "dm"]
 
 
 def rank_program(g, core, T, topo):
@@ -107,13 +123,20 @@ def rank_program(g, core, T, topo):
                 lastw[x[0]][c] = e
                 readers[x[0]][c] = None
 
+    calls = []
+
+    def later(q, issue, reads, writes):
+        calls.append((q, issue, reads, writes))
+
     def run(q, call, reads, writes):
         reads = [x for x in reads if isinstance(x, tuple)]
         reads = reads + [x[4] for x in reads + writes if x[4] is not None]
-        need(q, reads, writes)
-        cnt[q] += 1
-        call().then_inc(T.sem[q], 1)
-        note((q, cnt[q]), reads, writes)
+
+        def issue():
+            cnt[q] += 1
+            call().then_inc(T.sem[q], 1)
+            return q
+        later(q, issue, reads, writes)
 
     def copy(o, i):
         run("V", lambda: g.vector.tensor_copy(ap(o), ap(i)), [i], [o])
@@ -161,22 +184,24 @@ def rank_program(g, core, T, topo):
         kw = {} if SCRATCH[o[0]][2] == I32 else {"allow_small_or_imprecise_dtypes": True}
         run("G", lambda: g.iota(ap(o), pat, base, cm, **kw), [], [o])
 
-    def asel(o, i, pat, op, base, cm):
-        run("G", lambda: g.affine_select(ap(o), ap(i), pat, op, 0.0, base, cm), [i], [o])
+    def asel(o, i, pat, op, base, cm, fill=0.0):
+        run("G", lambda: g.affine_select(ap(o), ap(i), pat, op, fill, base, cm), [i], [o])
 
-    def load(q, o, src, sem, cast=None):
-        need(q, [], [o])
-        cnt[sem] += 16
-        Q[q].dma_start(ap(o, cast), src).then_inc(T.sem[sem], 16)
-        landed([o], sem)
+    def dma(q, pairs, sem, reads, writes):
+        def issue():
+            for o, i in pairs:
+                cnt[sem] += 16
+                Q[q].dma_start(o, i).then_inc(T.sem[sem], 16)
+            return sem
+        later(q, issue, reads, writes)
+
+    def load(q, o, src, sem, after=()):
+        dma(q, [(ap(o), src)], sem, list(after), [o])
 
     def store(q, dst, src, i):
-        need(q, [i], [])
-        cnt["oh"] += 16
-        Q[q].dma_start(dst, src).then_inc(T.sem.oh, 16)
+        dma(q, [(dst, src)], "oh", [i], [])
 
     def send(parts):
-        need("G", [p[0] for p in parts], [])
         trs = []
         for k, (s, d, r, sem) in enumerate(parts):
             dst = T.cores[r]
@@ -195,13 +220,19 @@ def rank_program(g, core, T, topo):
         if trs:
             g.remote_dma_fused(trs, local_sem=T.sem.sent)
 
-    def landed(views, sem):
-        note((sem, cnt[sem]), [], views)
+    def post(pairs, r, sem):
+        def issue():
+            for s, d in pairs:
+                send([(s, d, r, sem)])
+            return sem
+        later("G", issue, [p[0] for p in pairs], [p[1] for p in pairs])
 
     def cross(n, a, w, dests, sem):
-        for t in "qs":
-            send([(v(t + n, a, a + w), v(t + d, c, c + w), r, sem) for d, c, r in dests])
-        landed([v(t + d, c, c + w) for d, c, r in dests for t in "qs"], sem)
+        def issue():
+            for t in "qs":
+                send([(v(t + n, a, a + w), v(t + d, c, c + w), r, sem) for d, c, r in dests])
+            return sem
+        later("G", issue, [v(t + n, a, a + w) for t in "qs"], [v(t + d, c, c + w) for d, c, r in dests for t in "qs"])
 
     def cf(k):
         return v("cf", k, k + 1)
@@ -218,59 +249,59 @@ def rank_program(g, core, T, topo):
     load("S", v("tua"), T.ua[:], "dua")
     load("Y", v("tx", 768, 1536), T.x[:, 768:1536], "dx2")
     load("Y", v("tx", 0, 768), T.x[:, 0:768], "dx")
-    iota(ci(0), [[0, 1]], 0, 1)
+    iota(ci(0), [[0, 1]], int(12 * B), 1)
     iota(v("r16"), [[16, 24]])
-    iota(v("t2"), [[0, 24], [1, 16]])
     mset(v("ones"), 1.0)
     asel(v("e0"), v("ones"), [[1, 516]], A.is_equal, -3, -4)
-    ts(ci(1), ci(0), 15, A.bitwise_and)
-    ts(ci(2), ci(0), 2, A.arith_shift_right, 3, A.bitwise_and)
-    ts(ci(3), ci(0), 1, A.bitwise_and)
-    for u in (3, 4, 5):
-        mset(v("f%d" % u, 4 * FIRST[u]), 0.0)
+    for c in (0, 192):
+        iota(v("t2", c, c + 192), [[0, 12], [1, 16]])
+    pad("f5", FW[5], FIRST[5])
+    for k, m in ((1, 15), (2, 12), (3, int(12 * B) + 3), (4, 1)):
+        ts(ci(k), ci(0), m, A.bitwise_and)
     copy(v("pl"), v("r16", 0, 8))
-    copy(v("cf", 1, 4), v("ci", 1, 4))
-    act(cc(1), cf(1), F.Identity, scale=B - 1, bias=15 - 17 * B)
-    act(cc(4), cf(1), F.Identity, scale=-1.0, bias=0.5)
-    act(v("kk"), v("r16"), F.Identity, bias=cc(1))
-    ts(v("mN"), v("t2"), cf(1), A.not_equal, -BIG, A.mult)
-    quant("ua", 0, 128, v("tua"))
-    ts(v("mM"), v("t2"), -0.5, A.add, BIG, A.mult)
-    pick("sa", 0, 128, "ua", v("pl"))
-    act(v("mN0"), v("t2"), F.Sign, bias=cc(4))
-    act(v("m2"), v("mN0"), F.Identity, scale=B)
-    for u in (1, 0, 2):
+    for u in (4, 3):
         pad("f%d" % u, FW[u], FIRST[u])
+    copy(v("cf", 1, 5), v("ci", 1, 5))
+    for u in (2, 0):
+        act(v("f%d" % u, 4 * FIRST[u]), v("ones", 0, 192), F.Copy, scale=0.0)
+    act(cc(3), cf(1), F.Square, scale=-32.0, bias=480.0)
+    act(cc(4), cf(1), F.Identity, scale=-1.0, bias=15 - 2 * B)
+    act(cc(5), cf(1), F.Identity, scale=-2 * B, bias=B)
+    act(v("f1", 4 * FIRST[1]), v("ones", 0, 192), F.Copy, scale=0.0)
+    act(cc(1), cc(3), F.Identity, scale=-1.0, bias=cc(4))
+    ts(cc(2), cf(2), -B, A.mult, cf(3), A.add)
+    ts(cc(6), cf(4), 192.0, A.mult)
+    ts(cc(7), cf(4), -96.5, A.mult, 96.0, A.add)
+    quant("ua", 0, 128, v("tua"))
+    act(cc(8), cf(1), F.Identity, scale=0.5, bias=cc(7))
     asel(v("sgA"), v("ones", 0, 512), [[-16, 8], [0, 64]], A.is_ge, 0, 1)
-    asel(v("sgB"), v("sgA"), [[16, 8], [0, 64]], A.is_ge, 15, -1)
     iota(v("jj"), [[1, 384]])
-    pad("lo", 128, 96)
+    asel(v("sgB"), v("sgA"), [[16, 8], [0, 64]], A.is_ge, 15, -1)
+    pad("lo", 128, 96 - SPLIT[0] // 4)
+    pad("la", 128 - SPLIT[0] // 4, 0)
     pad("le", 32, 0)
-    pad("f6", 192, 144)
+    pad("f6", 192, 96)
+    pad("f7", 176, 80)
     pad("th1", 32, 0)
     pad("tm", 80, 0)
-    quant("x", 192, C, v("tx", 768, 1536))
-    mm(3, "sa", 0, "x", 256, C)
-    quant("x", 0, 192, v("tx", 0, 768))
-    need("Y", [v("tx")], [])
-    load("Y", v("qw2"), T.wc[:], "dw", dt.uint8)
-    load("Y", v("sw2"), T.ws[:], "dw")
-    landed([v("qw2")], "dw")
-    load("Y", v("tub"), T.ub[:], "dub")
-    load("Y", v("tv"), T.v[:], "dv")
+
+    def high0(k):
+        tt(v("th0", 384 * k, 384 * k + 384), v("dd0", ind=v("lw0", 24 + 48 * k, 48 + 48 * k)), v(("g30", "g10")[k]), A.subtract)
 
     def down(l, s, a):
         n = C >> l
         nb, h = n // 16, n // 4
-        tiles = ["f0", "f1", "f2", "f3", "f4", "f5"] if l == 0 else ["f6", "f4", "f5"]
-        wid = FW if l == 0 else FW[3:]
+        tiles = ["f0", "f1", "f2", "f3", "f4", "f5"] if l == 0 else ["f6", "f7", "f5"]
+        wid = FW if l == 0 else (192, 176, 128)
         off = [sum(wid[:u]) for u in range(len(wid))]
-        oo, rr, iu = C * l, "rr%d" % l, v("iu", 24 * l, 24 * l + nb)
-        lw, dd, g3 = "lw%d" % l, "dd%d" % l, "g3%d" % l
-        sr, ks = SR[l], min(SR[l])
+        oo, iu = C * l, v("iu", 24 * l, 24 * l + nb)
+        lw, dd, g3, g1 = "lw%d" % l, "dd%d" % l, "g3%d" % l, "g1%d" % l
+
+        def rsum(r):
+            return 118 + r if r > 16 else 144 + 12 * l + r
 
         def slot(r, w, first=0):
-            k = nb - r
+            k = SLOTS[l].index(r)
             return v(tiles[k // 4], 4 * first + k % 4, 4 * w, 4)
 
         def xx(a_, b_):
@@ -278,196 +309,216 @@ def rank_program(g, core, T, topo):
 
         def own(r):
             return v("px", 16 * r + 15, 16 * r + 16)
-        mm(1, s, 0, a, 0, n)
-        mm(0, s, 0, a, 0, n)
-        if l == 1:
-            for b in range(4):
-                mm(4 + b, "e", 128 * b, a, 0, n)
+
+        def sgn(r):
+            return v("sgn", 8 * r * (r - 1), 8 * r * (r + 1))
         done, z = [], (n, n)
         for x in VR[l]:
             if isinstance(x, int):
                 ts(slot(x, 16 * x), bank(0, 0, 16 * x), own(x), A.is_lt)
             elif x[0] == "o":
                 z = (int(x[1:]), z[0])
-                tt(v("d1", *z), bank(3, 64, 128) if z[0] == 320 else bank(1 if z[0] else 0, *z), v("mN", *z), A.add)
+                tt(v("d1", *z), bank(3, z[0] - 192, z[1] - 192) if z[0] >= 192 else bank(l, *z), v("mN", 0, z[1] - z[0]), A.subtract)
             elif x == "s":
-                scan(v("px", *z), v("mM", *z), v("d1", *z), A.min, A.max)
-            elif x == "S":
-                for k in range(len(sr) + 1):
-                    if k < len(sr):
-                        r = sr[k]
-                        act(v("sgn", 384 * k, 384 * k + 16 * r), bank(1, 0, 16 * r), F.Sign, bias=own(r), scale=-1.0)
-                    if k > 0:
-                        r = sr[k - 1]
-                        act(slot(r, 16 * r), v("sgn", 384 * (k - 1), 384 * (k - 1) + 16 * r), F.Relu, accum_out=v(rr, r, r + 1))
-            elif x == "R":
-                ts(v("mR"), v("t2"), 1.0, A.min)
+                scan(v("px", *z), v("mM", 0, z[1] - z[0]), v("d1", *z), A.min, A.max)
+            elif x[0] == "A":
+                r = int(x[1:])
+                act(sgn(r), bank(1, 0, 16 * r), F.Sign, bias=own(r), scale=-1.0)
+            elif x[0] == "B":
+                r = int(x[1:])
+                act(slot(r, 16 * r), sgn(r), F.Relu, accum_out=v("rr", rsum(r), rsum(r) + 1))
+            elif x == "u":
+                pick("sa", 0, 128, "ua", v("pl"))
+                act(v("kk"), v("r16"), F.Identity, bias=cc(1))
+                act(v("m2"), v("t2"), F.Identity, scale=2 * B, bias=cc(5))
+            elif x == "X":
+                quant("x", 192, C, v("tx", 768, 1536))
+                mm(3, "sa", 0, "x", 192, C)
+            elif x == "N":
+                ts(v("mN"), v("t2", 0, 192), cf(1), A.not_equal, BIG, A.mult)
+            elif x == "M":
+                act(v("mM"), v("t2", 0, 192), F.Identity, scale=BIG, bias=-0.5 * BIG)
+            elif x == "x":
+                quant("x", 0, 192, v("tx", 0, 768))
+                load("Y", v("tub"), T.ub[:], "dub", [v("tx")])
+                dma("Y", [(ap(v("qw2"), dt.uint8), T.wc[:]), (ap(v("sw2")), T.ws[:])], "dw", [v("tx")], [v("qw2"), v("sw2")])
+                load("Y", v("tv"), T.v[:], "dv", [v("tx")])
+            elif x == "H":
+                quant("h0", 0, 192, v("th0"))
+            elif x == "n":
+                quant("en", 0, 128, v("en0"))
+            elif x[0] == "m":
+                mm(int(x[1]), s, 0, a, 0, n)
             elif x == "g":
                 quant("sg", 0, 128, v("sgB"))
-            elif x == "i":
-                quant("v", 0, 128, v("tv"))
             elif x[0] == "e":
                 b = int(x[1])
                 quant("e", 128 * b, 128 * b + 128, v("e0", 3 - b, 515 - b))
-                mm(4 + b, "e", 128 * b, a, 0, n)
+            elif x == "E":
+                for b in (0, 2, 1, 3):
+                    mm(4 + b, "e", 128 * b, a, 0, n)
             elif x == "d":
                 tt(slot(nb, n), bank(0, 0, n), v("px", 0, n), A.is_le)
             elif x == "b":
-                scan(v("rb", 0, n), v("mR", 0, n), slot(nb, n), A.mult, A.add)
+                scan(v("rb", 0, n), v("t2", 0, n), slot(nb, n), A.min, A.add)
             elif x == "k":
                 tt(xx(0, nb), v("kk", 0, nb), v("rb", 15, n, 16), A.subtract)
-            elif x == "w":
-                tt(xx(ks, nb), xx(ks, nb), v(rr, ks, nb), A.subtract)
-            elif x == "v":
-                tt(xx(1, ks), xx(1, ks), v("rs", 383, 192 * ks, 192), A.subtract)
+            elif x[0] in "wv":
+                a_, b_ = (int(y) for y in x[1:].split("-"))
+                tt(xx(a_, b_), xx(a_, b_), v("rr", rsum(a_), rsum(b_ - 1) + 1) if x[0] == "w" else v("rs", 192 * a_ + 191, 192 * b_, 192),
+                   A.subtract)
+            elif x[0] == "p":
+                a_, b_ = ((0, LATE[l]), (LATE[l], n))[int(x[1])]
+                part = v("iu", 24 * l + a_ // 16, 24 * l + b_ // 16)
+                scan(v("sel", a_, b_), bank(3 - int(x[1]), a_, b_), v("m2", a_, b_), A.max, A.add)
+                ts(part, v("sel", a_ + 15, b_, 16), 2 * B, A.add)
+                copy(v("oo", oo, oo + n, ind=part), v("jj", a_, b_))
             elif x[0] == "r":
                 r = int(x[1:])
-                scan(v("rs", 184 * r + 192, 192 * r + 192), slot(r, 8 * r), slot(r, 16 * r, 8 * r), A.add, A.add)
+                scan(v("rs", 184 * r + 192, 192 * r + 192) if r < 17 else v("rr", 0, 136), slot(r, 8 * r), slot(r, 16 * r, 8 * r), A.add, A.add)
             else:
                 u = int(x[1:])
                 quant("f", off[u], off[u] + wid[u], v(tiles[u]))
-                mm(2, "sg", 0, "f", off[u], off[u] + wid[u], not done, len(done) == len(tiles) - 1)
+                if wid[u] > LATE[l]:
+                    mm(2, "sg", 0, "f", off[u], off[u] + wid[u], not done, u == 1)
+                mm(3, "sg", 0, "f", off[u], off[u] + min(wid[u], LATE[l]), not done, len(done) == len(tiles) - 1)
                 done.append(u)
-        if l == 0:
-            act(cc(9), cf(2), F.Identity, scale=4.0, bias=2.0)
-            act(cc(8), cf(2), F.Identity, scale=-4 * B - 4, bias=12 * B)
-            act(v("t4"), v("t2", 0, 384, 4), F.Sign, bias=cc(9), scale=-1.0)
-            act(cc(2), cc(8), F.Identity, bias=cf(1))
-            act(v("m4"), v("t4"), F.Identity, bias=1.5 * B, scale=2.5 * B)
         for b in (0, 2, 1, 3):
             act(v(dd, b, 4 * n, 4), bank(4 + b, 0, n), F.Copy, scale=0.5)
-        scan(v("sel", 0, n), bank(2, 0, n), v("m2", 0, n), A.max, A.add)
-        ts(iu, v("sel", 15, n, 16), 2 * B, A.add)
-        if l == 1:
-            ts(v("iw1"), v("sel", 15, n, 16), 2 * B, A.add)
-            send([(v("iw1"), v("lland"), rank ^ 1, "al")])
-            landed([v("lland")], "al")
-        copy(v("oo", oo, oo + n, ind=iu), v("jj", 0, n))
-        scans(l, 0)
-        lists(l, 0)
-        move("S", v(g3, n // 2, n), v(dd, ind=v(lw, nb // 2, nb)))
-        move("V", v(g3, 0, n // 2), v(dd, ind=v(lw, 0, nb // 2)))
         if l == 0:
+            asel(v("en0"), v("e0", 0, 512), [[1, 512]], A.not_equal, -3, -4, -1.0)
+            ts(v("t4"), v("t2", 0, 384, 4), cf(2), A.is_le, 5 * B, A.mult)
             quant("ub", 0, 128, v("tub"))
+            quant("v", 0, 128, v("tv"))
+            pick("sb", 0, 128, "ub", v("pl"))
+            ts(v("m4"), v("t4"), -B, A.add)
+            ts(v("nat"), v("r16", 0, 12), 0.5, A.mult, cc(8), A.add)
         else:
-            scans(l, 2)
-        tt(v("lo", 0, n // 2), v(dd, ind=v(lw, nb, 3 * nb // 2)), v(g3, 0, n // 2), A.add)
-        if l == 1:
-            lists(l, 2)
-            move("S", v("g11"), v(dd, ind=v(lw, 2 * nb, 3 * nb)))
-        tt(v("lo", n // 2, n), v(dd, ind=v(lw, 3 * nb // 2, 2 * nb)), v(g3, n // 2, n), A.add)
-        quant("lo%d" % l, 0, 128, v("lo"))
-        cross("lo%d" % l, 0, h, [("l%d" % l, 128, rank ^ (1 << l))], "a%d" % l)
+            pick("hn", 0, 192, "h0", v("nat"))
+            post([(iu, v("lland"))], rank ^ 1, "al")
+        for k in range(4):
+            scan(v("sw", k * h, (k + 1) * h), v("m4", 0, h), v("oo", oo + 3 - k, oo + n, 4), A.add, A.min)
+        for k in (0, 2):
+            ts(v(lw, k * nb, (k + 2) * nb), v("sw", k * h + 3, (k + 2) * h, 4), 4.0, A.mult, cc(2), A.add)
+        c = SPLIT[l]
+        move("S", v(g3, c, n), v(dd, ind=v(lw, c // 16, nb)))
+        move("V", v(g3, 0, c), v(dd, ind=v(lw, 0, c // 16)))
+        move("S", v(g1, 0, n), v(dd, ind=v(lw, 2 * nb, 3 * nb)))
+        tt(v("lo", 0, c) if l else v("la", 512 - c, 512), v(dd, ind=v(lw, nb, nb + c // 16)), v(g3, 0, c), A.add)
+        if l == 0:
+            quant("lo0", 0, 128, v("la"))
+            post([(v("qlo0", 128 - c // 4, 128), v("ql0", 128, 128 + c // 4))], rank ^ 1, "a9")
+        tt(v("lo", c, n) if l else v("lo", 0, n - c), v(dd, ind=v(lw, nb + c // 16, 2 * nb)), v(g3, c, n), A.add)
+        tt(v("le", 512 - n, 512), v(dd, ind=v(lw, 3 * nb, 4 * nb)), v(g1), A.add)
+        if l:
+            quant("lo1", 0, 128, v("lo"))
+            cross("lo1", 0, h, [("l1", 128, rank ^ 2)], "a1")
+        else:
+            quant("lo0", 128, 256, v("lo"))
+            post([(v("qlo0", 128, 224 - c // 4), v("ql0", 128 + c // 4, 224)), (v("slo0", 128 - c // 4, 224 - c // 4), v("sl0", 128, 224))],
+                 rank ^ 1, "a0")
 
-    def scans(l, k0):
-        n = C >> l
-        for k in (k0, k0 + 1):
-            scan(v("sw", k * n // 4, (k + 1) * n // 4), v("m4", 0, n // 4), v("oo", C * l + 3 - k, C * l + n, 4), A.add, A.min)
-
-    def lists(l, k0):
-        h, nb = 96 >> l, 24 >> l
-        ts(v("lw%d" % l, k0 * nb, (k0 + 2) * nb), v("sw", k0 * h + 3, (k0 + 2) * h, 4), 4.0, A.mult, cc(2), A.add)
-
-    def layer(x, a, k0, h, out):
+    def layer(x, a, k0, h, out, qs="VVVV"):
         for b in range(4):
             mm(k0 + b, "w2", 128 * b, x, a, a + 128)
         for b in range(4):
-            move("V", out(b), bank(k0 + b, 128 - h, 128), 0.03125)
+            move(qs[b], out(b), bank(k0 + b, 128 - h, 128), 0.03125)
 
     down(0, "sa", "x")
-    scans(0, 2)
-    lists(0, 2)
-    move("S", v("g10", 192, 384), v("dd0", ind=v("lw0", 60, 72)))
-    move("V", v("g10", 0, 192), v("dd0", ind=v("lw0", 48, 60)))
-    pick("sb", 0, 128, "ub", v("pl"))
-    act(cc(6), cf(3), F.Copy, scale=192.0)
-    act(v("en0"), v("e0"), F.Copy, scale=-1.0)
-    tt(v("le", 128, 512), v("dd0", ind=v("lw0", 72, 96)), v("g10"), A.add)
+    high0(0)
     quant("l0", 0, 128, v("le"))
-    layer("l0", 0, 0, 96, lambda b: v("ta1", b, 768, 8))
-    layer("l0", 96, 4, 96, lambda b: v("ta1", 4 + b, 768, 8))
+    high0(1)
+    layer("l0", 0, 0, 96, lambda b: v("ta1", b, 768, 8), "SSSS")
+    layer("l0", 96, 4, 96, lambda b: v("ta1", 4 + b, 768, 8), "VSVV")
     quant("a1", 0, 192, v("ta1"))
 
     down(1, "sb", "a1")
     store("Y", T.ol[:], T.oo[0:128:16, :], v("oo"))
-    need("Y", [v("iw1")], [v("lland")])
-    cnt["dm"] += 16
-    g.sync.dma_start(T.lland[0:128:2, :], T.iw1[0:128:2, :]).then_inc(T.sem.dm, 16)
-    landed([v("lland")], "dm")
-    tt(v("th1", 320, 512), v("dd1", ind=v("lw1", 12, 24)), v("g31"), A.subtract)
-    tt(v("le", 320, 512), v("dd1", ind=v("lw1", 36, 48)), v("g11"), A.add)
-    tt(v("th1", 128, 320), v("dd1", ind=v("lw1", 36, 48)), v("g11"), A.subtract)
+    dma("Y", [(T.lland[0:128:2, :], T.iu[0:128:2, 24:36])], "dm", [v("iu", 24, 36)], [v("lland")])
     quant("l1", 0, 128, v("le"))
+    tt(v("th1", 320, 512), v("dd1", ind=v("lw1", 12, 24)), v("g31"), A.subtract)
+    tt(v("th1", 128, 320), v("dd1", ind=v("lw1", 36, 48)), v("g11"), A.subtract)
     for b in range(4):
         mm(b, "w2", 128 * b, "l1", 0, 128)
-    quant("hh", 0, 128, v("th1"))
-    cross("hh", 32, 96, [("hh", 128, rank ^ 1)], "ah")
     for b in range(4):
-        move("V", v("tm", 320 + b, 512, 4), bank(b, 80, 128), 0.03125)
+        move("SSSV"[b], v("tm", 320 + b, 512, 4), bank(b, 80, 128), 0.03125)
+        if b == 0:
+            quant("hh", 0, 128, v("th1"))
+            cross("hh", 32, 96, [("hh", 128, rank ^ 1)], "ah")
+    copy(v("yw"), v("lland"))
     quant("st", 0, 128, v("tm"))
     cross("st", 80, 48, [("st", 176, rank ^ 1)], "am")
+    ts(v("yi"), v("yw"), 3, A.bitwise_and)
     layer("l1", 48, 4, 48, lambda b: v("lo", b, 192, 4))
+    ts(v("yf", 0, 12), v("yi"), 2.0, A.is_ge, 188.0, A.mult)
+    tt(v("yf", 12, 24), v("yi"), v("yw"), A.add)
     quant("a2", 0, 128, v("lo"))
     cross("a2", 0, 48, [("st", 128, rank ^ 2), ("st", 224, rank ^ 3)], "a2")
 
-    def pair(w, d, b, k):
+    def pair(w, d, b, k, a=0, e=192, c=0):
         for s, op in enumerate((A.add, A.subtract)):
-            tt(v(w, 384 * b + s, 384 * b + 384, 2), bank(k, 0, 192), v(d, 192 * b, 192 * b + 192), op)
-    for b in (2, 3):
-        quant("en", 128 * b, 128 * b + 128, v("en0", 3 - b, 515 - b))
-    for b in range(2):
-        mm(b, "e", 128 * b, "hh", 32, 224)
-    for k in range(4):
-        mm(4 + k, ("e", "en")[k & 1], 256 + 128 * (k // 2), "hh", 32, 224, True, False)
-    for b in range(2):
-        move("S", v("dh1", 192 * b, 192 * b + 192), bank(b, 0, 192))
-    tt(v("th0", 0, 384), v("dd0", ind=v("lw0", 24, 48)), v("g30"), A.subtract)
-    ts(v("yi"), v("lland"), 3, A.bitwise_and)
-    tt(v("th0", 384, 768), v("dd0", ind=v("lw0", 72, 96)), v("g10"), A.subtract)
-    ts(v("yf", 0, 12), v("yi"), 2.0, A.is_ge, 188.0, A.mult)
-    tt(v("yf", 12, 24), v("yi"), v("lland"), A.add)
-    quant("h0", 0, 192, v("th0"))
+            tt(v(w, 384 * b + 2 * a + s, 384 * b + 2 * e, 2), bank(k, c, c + e - a), v(d, 192 * b + a, 192 * b + e), op)
+
+    def both(k, x, a, first):
+        for s in range(2):
+            mm(k + s, ("e", "en")[s if first else 0], 0 if first and s else 384, x, a, a + 192, first, not first)
     tt(v("yf", 24, 36), v("yf", 0, 12), v("yf", 12, 24), A.add)
     ts(v("c1"), v("yf", 24, 36), 0.5, A.mult, cc(6), A.add)
-    for k in (0, 4, 5, 1, 6, 7):
-        mm(k, "e", 128 * k if k < 4 else 128 * (k // 2), "st", 80, 272, k < 4, True)
-    for b in (2, 3):
-        mm(b, "e", 128 * b, "h0", 0, 192)
-    pair("w1", "dh1", 0, 0)
-    pair("w1", "dh1", 1, 1)
-    for k in range(4):
-        move("S", v("w1", 768 + 384 * (k // 2) + k % 2, 1152 + 384 * (k // 2), 2), bank(4 + k, 0, 192))
-    for b in (0, 2, 1):
-        move("VVS"[b], v("ta3", b, 768, 4), v("w1", 384 * b, 384 * b + 384, ind=v("c1")))
-    move("S", v("ta3", 3, 384, 4), v("w1", 1152, 1536, ind=v("c1", 0, 6)))
-    move("V", v("ta3", 387, 768, 4), v("w1", 1152, 1536, ind=v("c1", 6, 12)))
-    for b in (0, 1):
-        mm(4 + b, "e", 128 * b, "h0", 0, 192)
-    for b, k in ((0, 4), (1, 5), (2, 2), (3, 3)):
-        move("S", v("dh0", 192 * b + 1, 192 * b + 192, 2), bank(k, 0, 96))
-        move("S", v("dh0", 192 * b, 192 * b + 192, 2), bank(k, 96, 192))
+    for b in range(3):
+        mm(b, "e", 128 * b, "hh", 32, 224)
+    both(3, "hh", 32, True)
+    both(5, "hn", 0, True)
+    for b in range(3):
+        move("S", v("dh1", 192 * b, 192 * b + 192), bank(b, 0, 192))
+    mm(2, "e", 0, "hn", 0, 192)
+    move("S", v("dh0", 0, 192), bank(2, 0, 192))
+    for b in range(3):
+        mm((7, 0, 1)[b], "e", 128 * b, "st", 0, 128)
+        pair("w1", "dh1", b, (7, 0, 1)[b], 0, 48, 80)
+    mm(7, "e", 0, "st", 128, 272)
+    both(3, "st", 80, False)
+    for b in (1, 2):
+        mm(b - 1, "e", 128 * b, "st", 128, 272)
+    for b in range(3):
+        pair("w1", "dh1", b, (7, 0, 1)[b], 48, 192)
+    for k in range(2):
+        move("S", v("w1", 1152 + k, 1536, 2), bank(3 + k, 0, 192))
+    for b in (1, 2):
+        mm(b - 1, "e", 128 * b, "hn", 0, 192)
+        move("S", v("dh0", 192 * b, 192 * b + 192), bank(b - 1, 0, 192))
+    for x in UP1:
+        b, a, e = int(x[1]), (0, 0, 6)[int(x[2])], (12, 6, 12)[int(x[2])]
+        move(x[0], v("ta3", 64 * a + b, 64 * e, 4), v("w1", 384 * b, 384 * b + 384, ind=v("c1", a, e)))
     quant("a3", 0, 192, v("ta3"))
 
-    for b in range(4):
-        mm((0, 1, 6, 7)[b], "e", 128 * b, "a3", 0, 192)
-    for b in range(4):
-        pair("w0", "dh0", b, (0, 1, 6, 7)[b])
+    mm(7, "e", 0, "a3", 0, 192)
+    both(5, "a3", 0, False)
+    for b in (1, 2):
+        mm(b + 1, "e", 128 * b, "a3", 0, 192)
+    for b in range(3):
+        pair("w0", "dh0", b, (7, 2, 3)[b])
+    for k in range(2):
+        move("S", v("w0", 1152 + k, 1536, 2), bank(5 + k, 0, 192))
     for x in TAIL:
-        a, e = ((0, CUT), (CUT, C))[x[-1] == "1"]
+        u = int(x[-1])
+        a, e = CUTS[u], CUTS[u + 1]
         if x[0] == "f":
             quant("fin", a, e, v("tf", 4 * a, 4 * e))
-            mm(4 + int(x[1]), "v", 0, "fin", a, e)
+            mm(4 - 4 * u, "v", 0, "fin", a, e)
             store("Y", T.oc[:, 4 * a:4 * e], T.qfin[:, a:e].bitcast(dt.uint8), v("qfin", a, e))
-        elif x == "y":
-            move("S", v("ty", 0, CUT), bank(4, 0, CUT))
+            if e == C:
+                dma("Y", [(T.osc[4 * k:4 * k + 4, :], T.sfin[32 * k:32 * k + 4, :]) for k in range(4)], "oh", [v("sfin")], [])
+        elif x[0] == "y":
+            move(x[1], v("ty", a, e), bank(4 - 4 * u, 0, e - a))
+            store("S", T.y[:, a:e], T.ty[:, a:e], v("ty", a, e))
         else:
             b = int(x[1])
             move(x[0], v("tf", 4 * a + b, 4 * e, 4), v("w0", 384 * b, 384 * b + 384, ind=v("iu", a // 16, e // 16)))
-    move("V", v("ty", CUT, C), bank(5, 0, C - CUT))
-    store("S", T.y[:, 0:CUT], T.ty[:, 0:CUT], v("ty", 0, CUT))
-    for k in range(4):
-        store("Y", T.osc[4 * k:4 * k + 4, :], T.sfin[32 * k:32 * k + 4, :], v("sfin"))
-    store("S", T.y[:, CUT:C], T.ty[:, CUT:C], v("ty", CUT, C))
+    for k in ORDER or range(len(calls)):
+        q, issue, reads, writes = calls[k]
+        need(q, reads, writes)
+        e = issue()
+        note((e, cnt[e]), reads if e in Q else [], writes)
     for n in SEMAPHORES:
         if cnt[n] and seen["G"].get(n, 0) < cnt[n]:
             g.wait_ge(T.sem[n], cnt[n])

from concourse.bass import DstId, RemoteDMATransfer
from concourse.mybir import dt, AluOpType as A, ActivationFunctionType as F

SLOTS = (tuple(range(24, 0, -1)), (12, 8, 7, 6, 11, 10, 9, 5, 4, 3, 2, 1))
LATE = (160, 192)
C = 384
ORDER = tuple(int(_k) for _k in """
5 3 0 1 2 4 7 10 11 12 13 17 25 26 14 27 28 47 40 19 23 22 20 21 29 24 41 18 42 53 6 8 43 44 45 48 57 49 55 66 54 149 71 58 59 46 50 51 52 56
16 9 30 32 15 31 33 34 35 36 75 63 65 60 72 61 73 64 62 94 79 81 91 82 85 76 77 74 84 83 78 123 99 121 120 95 124 96 80 128 112 130 101 89 122
114 92 131 129 100 90 93 102 113 104 108 109 97 103 98 117 107 127 132 126 125 88 87 86 139 137 70 69 67 106 105 110 111 116 115 118 119 133
138 68 134 140 150 135 141 136 142 154 147 146 144 145 143 156 157 158 160 163 153 162 159 165 161 166 168 151 170 167 171 148 37 38 39 164 169
173 175 179 177 181 176 178 180 182 152 155 172 185 184 189 186 190 188 183 187 191 192 199 193 195 196 197 194 200 201 213 216 210 209 215 214
202 204 203 205 207 206 219 211 229 208 232 230 231 212 225 217 220 226 223 224 222 228 234 240 241 238 239 233 218 221 227 235 236 237 245 244
246 247 249 248 259 260 252 250 251 253 254 255 257 256 263 261 262 269 258 265 267 266 264 271 272 268 270 278 279 281 280 273 174 275 282 283
285 284 288 292 276 299 274 277 198 286 287 304 293 294 296 307 289 305 306 242 300 309 290 310 295 301 243 312 311 308 291 313 315 318 319 325
317 314 324 331 322 323 316 320 321 330 332 333 297 298 302 326 328 303 327 329 334 335 340 336 338 341 343 342 346 337 339 345 344 347 349 350
348 351 358 353 354 356 352 355 357 361 363 364 359 360 362 365 366
""".split())
BIG = float(2 ** 80)
B = 1024.0
VR = (("u", "X", "e0", "N", "e2", "x", "M", "o320", "m1", "m0", "e1", "e3", "s", "A23", "A22", "B23", "A21", "B22", "A20", "o192", "E", "s",
       "B21", "A19", "B20", "A18", "B19", "B18", 17, "o0", 16, 15, "s", "A8", "A7", "A6", "B8", "B7", "B6", 14, "r17", 13, "d", "r16", 12,
       "r15", 11, "r14", "b", 10, "r13", 9, "g", "r12", "q0", "k", "r11", "q2", "r10", "r9", "q3", "q1", 5, 4, 3, 2, 1, "w17-24", "v9-17",
       "r5", "r4", "r3", "r2", "r1", "q5", "p1", "q4", "v1-6", "w6-9", "p0"),
      ("m1", "m0", "E", "H", "n", "o0", "s", "A11", "A10", "A9", "B11", "B10", "B9", 8, 7, "d", 6, 5, 4, 3, 2, 1, "q0", "b", "q2", "r8", "r7",
       "k", "r6", "q1", "r5", "r4", "r3", "r2", "r1", "v1-9", "w9-12", "p0"))
UP1 = ("S30", "S00", "V20", "V10")
TAIL = ("V10", "S00", "S30", "V20", "S01", "f0", "S31", "V21", "V11", "yS0", "f1", "yV1")
CUTS = (0, 256, 384)
FW = (384, 320, 256, 192, 128, 128)
FIRST = (336, 272, 208, 144, 80, 16)
SPLIT = (128, 96)

S_, BF, F32, I32, U16, Q4, U8 = "sbuf", "bfloat16", "float32", "int32", "uint16", "float8_e4m3fn_x4", "uint8"
SCRATCH = {"ps": ("psum", [128, 4096], F32)}
for _d, _l in [
    (BF, "tx 1536 tua 512 tub 512 tv 512 t2 384 t4 96 ones 516 sgA 512 sgB 512 e0 516 en0 512 mM 192 mN 192 m4 96 rb 384 "
         "rs 3264 sgn 4416 f0 1536 f1 1280 f2 1024 f3 768 f4 512 f5 512 f6 768 f7 704 dd0 1536 dd1 768 g30 384 g10 384 g31 192 g11 192 lo 512 "
         "la 512 le 512 th0 768 ta1 768 tm 512 th1 512 dh0 576 dh1 576 ta3 768 tf 1536 w1 1536 w0 1536"),
    (F32, "cf 8 cc 12 r16 24 jj 384 m2 384 kk 24 d1 384 px 384 rr 168 sel 384 oo 576 sw 384 ty 384 yf 36"),
    (I32, "ci 8 yw 12 yi 12"),
    (U16, "pl 8 iu 36 lw0 96 lw1 48 c1 12 lland 12 nat 12"),
    (Q4, "x 384 ua 128 ub 128 v 128 sa 128 sb 128 w2 512 e 512 en 128 sg 128 f 1408 lo0 256 l0 224 lo1 128 l1 176 h0 192 hn 192 "
         "a1 192 hh 224 st 272 a2 128 a3 192 fin 384"),
]:
    for _n, _w in zip(_l.split()[::2], _l.split()[1::2]):
        if _d == Q4:
            SCRATCH["q" + _n] = (S_, [128, int(_w)], Q4)
            SCRATCH["s" + _n] = (S_, [128, int(_w)], U8)
        else:
            SCRATCH[_n] = (S_, [128, int(_w)], _d)

SEMAPHORES = ["V", "S", "P", "G", "dx", "dx2", "dua", "dub", "dv", "dw", "sent", "a0", "a9", "a1", "am", "ah", "al", "a2", "oh", "dm"]


def rank_program(g, core, T, topo):
    rank = T.rank_of(core)
    if rank is None:
        return
    Q = {"V": g.vector, "S": g.scalar, "P": g.tensor, "G": g, "Y": g.sync}
    cnt = {n: 0 for n in SEMAPHORES}
    seen = {q: {} for q in Q}
    lastw = {n: [None] * SCRATCH[n][1][1] for n in SCRATCH}
    readers = {n: [None] * SCRATCH[n][1][1] for n in SCRATCH}

    def v(n, a=0, b=None, s=1, ind=None):
        return (n, a, SCRATCH[n][1][1] if b is None else b, s, ind)

    def bank(k, a, b, s=1):
        return v("ps", 512 * k + a, 512 * k + b, s)

    def ap(x, cast=None):
        if not isinstance(x, tuple):
            return x
        n, a, b, s, ind = x
        r = T[n][:, a:b] if s == 1 else T[n][:, a:b:s]
        if cast is not None:
            r = r.bitcast(cast)
        if ind is not None:
            r = r.indirect(ap(ind))
        return r

    def cols(x):
        n, a, b, s, ind = x
        if n == "ps":
            return range(a // 512 * 512, a // 512 * 512 + 512, 512)
        return range(a, b, s)

    def need(q, reads, writes):
        ev = {}

        def add(e):
            if e is not None and ev.get(e[0], 0) < e[1]:
                ev[e[0]] = e[1]
        for x in reads:
            for c in cols(x):
                add(lastw[x[0]][c])
                if x[0] == "ps" and readers["ps"][c]:
                    for s2, n2 in readers["ps"][c].items():
                        if s2 != q:
                            add((s2, n2))
        for x in writes:
            for c in cols(x):
                e = lastw[x[0]][c]
                if e is not None and not (e[0] == q == "P"):
                    add(e)
                if readers[x[0]][c]:
                    for e in readers[x[0]][c].items():
                        add(e)
        for s2, n2 in ev.items():
            if seen[q].get(s2, 0) < n2:
                Q[q].wait_ge(T.sem[s2], n2)
                seen[q][s2] = n2

    def note(e, reads, writes):
        for x in reads:
            for c in cols(x):
                if readers[x[0]][c] is None:
                    readers[x[0]][c] = {}
                readers[x[0]][c][e[0]] = e[1]
        for x in writes:
            for c in cols(x):
                lastw[x[0]][c] = e
                readers[x[0]][c] = None

    calls = []

    def later(q, issue, reads, writes):
        calls.append((q, issue, reads, writes))

    def run(q, call, reads, writes):
        reads = [x for x in reads if isinstance(x, tuple)]
        reads = reads + [x[4] for x in reads + writes if x[4] is not None]

        def issue():
            cnt[q] += 1
            call().then_inc(T.sem[q], 1)
            return q
        later(q, issue, reads, writes)

    def copy(o, i):
        run("V", lambda: g.vector.tensor_copy(ap(o), ap(i)), [i], [o])

    def tt(o, a, b, op):
        run("V", lambda: g.vector.tensor_tensor(ap(o), ap(a), ap(b), op), [a, b], [o])

    def ts(o, a, s1, op0, s2=None, *op1):
        run("V", lambda: g.vector.tensor_scalar(ap(o), ap(a), ap(s1), ap(s2), op0, *op1), [a, s1, s2], [o])

    def scan(o, a, b, op0, op1):
        run("V", lambda: g.vector.tensor_tensor_scan(ap(o), ap(a), ap(b), 0.0, op0, op1), [a, b], [o])

    def mset(o, c):
        run("V", lambda: g.vector.memset(ap(o), c), [], [o])

    def act(o, i, fn, **kw):
        acc = kw.get("accum_out")
        run("S", lambda: g.scalar.activation(ap(o), ap(i), fn, **{k: ap(x) for k, x in kw.items()}),
            [i, kw.get("bias"), kw.get("scale")], [o] + ([acc] if acc else []))

    def move(q, o, i, scale=None):
        if q == "S":
            act(o, i, F.Copy, **({} if scale is None else {"scale": scale}))
        elif scale is None:
            copy(o, i)
        else:
            ts(o, i, scale, A.mult)

    def quant(n, a, b, i):
        o = [v("q" + n, a, b), v("s" + n, a, b)]
        run("V", lambda: g.vector.quantize_mx(ap(o[0]), ap(o[1]), ap(i)), [i], o)

    def mm(k, w, wa, x, a, b, start=True, stop=True):
        r = [v("q" + w, wa, wa + 128), v("s" + w, wa, wa + 128), v("q" + x, a, b), v("s" + x, a, b)]
        o = bank(k, 0, b - a)
        run("P", lambda: g.tensor.matmul_mx(ap(o), ap(r[0]), ap(r[1]), ap(r[2]), ap(r[3]), start, stop), r, [o])

    def pick(o, a, b, src, lst):
        oc_, ic = v("q" + o, a, b), v("q" + src, ind=lst)
        run("V", lambda: g.vector.tensor_copy(ap(oc_, dt.uint32), ap(ic, dt.uint32)), [ic], [oc_])
        act(v("s" + o, a, b), v("s" + src, ind=lst), F.Copy)

    def iota(o, pat, base=0, cm=0):
        kw = {} if SCRATCH[o[0]][2] == I32 else {"allow_small_or_imprecise_dtypes": True}
        run("G", lambda: g.iota(ap(o), pat, base, cm, **kw), [], [o])

    def asel(o, i, pat, op, base, cm, fill=0.0):
        run("G", lambda: g.affine_select(ap(o), ap(i), pat, op, fill, base, cm), [i], [o])

    def dma(q, pairs, sem, reads, writes):
        def issue():
            for o, i in pairs:
                cnt[sem] += 16
                Q[q].dma_start(o, i).then_inc(T.sem[sem], 16)
            return sem
        later(q, issue, reads, writes)

    def load(q, o, src, sem, after=()):
        dma(q, [(ap(o), src)], sem, list(after), [o])

    def store(q, dst, src, i):
        dma(q, [(dst, src)], "oh", [i], [])

    def send(parts):
        trs = []
        for k, (s, d, r, sem) in enumerate(parts):
            dst = T.cores[r]
            eng = topo.engines(core, dst)
            share = len(eng) // len(parts)
            mask = sum(1 << e for e in eng[k * share:(k + 1) * share])
            cast = dt.uint8 if SCRATCH[s[0]][2] == Q4 else None
            rid, pid = topo.addr(dst)[:2]
            cnt["sent"] += share
            cnt[sem] += share
            if len(parts) == 1:
                g.remote_dma(ap(d, cast), ap(s, cast), T.sem[sem], T.sem.sent, pid, rid, mask)
            else:
                trs.append(RemoteDMATransfer(dst_ids=[DstId(rid=rid, pnc=pid)], dma_engine_mask=mask, remote_sem=T.sem[sem],
                                             src=ap(s, cast), dst=ap(d, cast)))
        if trs:
            g.remote_dma_fused(trs, local_sem=T.sem.sent)

    def post(pairs, r, sem):
        def issue():
            for s, d in pairs:
                send([(s, d, r, sem)])
            return sem
        later("G", issue, [p[0] for p in pairs], [p[1] for p in pairs])

    def cross(n, a, w, dests, sem):
        def issue():
            for t in "qs":
                send([(v(t + n, a, a + w), v(t + d, c, c + w), r, sem) for d, c, r in dests])
            return sem
        later("G", issue, [v(t + n, a, a + w) for t in "qs"], [v(t + d, c, c + w) for d, c, r in dests for t in "qs"])

    def cf(k):
        return v("cf", k, k + 1)

    def cc(k):
        return v("cc", k, k + 1)

    def ci(k):
        return v("ci", k, k + 1)

    def pad(name, w, first):
        iota(v(name, 4 * first, 4 * w), [[0, 4 * (w - first)]])

    load("S", v("tua"), T.ua[:], "dua")
    load("Y", v("tx", 768, 1536), T.x[:, 768:1536], "dx2")
    load("Y", v("tx", 0, 768), T.x[:, 0:768], "dx")
    iota(ci(0), [[0, 1]], int(12 * B), 1)
    iota(v("r16"), [[16, 24]])
    mset(v("ones"), 1.0)
    asel(v("e0"), v("ones"), [[1, 516]], A.is_equal, -3, -4)
    for c in (0, 192):
        iota(v("t2", c, c + 192), [[0, 12], [1, 16]])
    pad("f5", FW[5], FIRST[5])
    for k, m in ((1, 15), (2, 12), (3, int(12 * B) + 3), (4, 1)):
        ts(ci(k), ci(0), m, A.bitwise_and)
    copy(v("pl"), v("r16", 0, 8))
    for u in (4, 3):
        pad("f%d" % u, FW[u], FIRST[u])
    copy(v("cf", 1, 5), v("ci", 1, 5))
    for u in (2, 0):
        act(v("f%d" % u, 4 * FIRST[u]), v("ones", 0, 192), F.Copy, scale=0.0)
    act(cc(3), cf(1), F.Square, scale=-32.0, bias=480.0)
    act(cc(4), cf(1), F.Identity, scale=-1.0, bias=15 - 2 * B)
    act(cc(5), cf(1), F.Identity, scale=-2 * B, bias=B)
    act(v("f1", 4 * FIRST[1]), v("ones", 0, 192), F.Copy, scale=0.0)
    act(cc(1), cc(3), F.Identity, scale=-1.0, bias=cc(4))
    ts(cc(2), cf(2), -B, A.mult, cf(3), A.add)
    ts(cc(6), cf(4), 192.0, A.mult)
    ts(cc(7), cf(4), -96.5, A.mult, 96.0, A.add)
    quant("ua", 0, 128, v("tua"))
    act(cc(8), cf(1), F.Identity, scale=0.5, bias=cc(7))
    asel(v("sgA"), v("ones", 0, 512), [[-16, 8], [0, 64]], A.is_ge, 0, 1)
    iota(v("jj"), [[1, 384]])
    asel(v("sgB"), v("sgA"), [[16, 8], [0, 64]], A.is_ge, 15, -1)
    pad("lo", 128, 96 - SPLIT[0] // 4)
    pad("la", 128 - SPLIT[0] // 4, 0)
    pad("le", 32, 0)
    pad("f6", 192, 96)
    pad("f7", 176, 80)
    pad("th1", 32, 0)
    pad("tm", 80, 0)

    def high0(k):
        tt(v("th0", 384 * k, 384 * k + 384), v("dd0", ind=v("lw0", 24 + 48 * k, 48 + 48 * k)), v(("g30", "g10")[k]), A.subtract)

    def down(l, s, a):
        n = C >> l
        nb, h = n // 16, n // 4
        tiles = ["f0", "f1", "f2", "f3", "f4", "f5"] if l == 0 else ["f6", "f7", "f5"]
        wid = FW if l == 0 else (192, 176, 128)
        off = [sum(wid[:u]) for u in range(len(wid))]
        oo, iu = C * l, v("iu", 24 * l, 24 * l + nb)
        lw, dd, g3, g1 = "lw%d" % l, "dd%d" % l, "g3%d" % l, "g1%d" % l

        def rsum(r):
            return 118 + r if r > 16 else 144 + 12 * l + r

        def slot(r, w, first=0):
            k = SLOTS[l].index(r)
            return v(tiles[k // 4], 4 * first + k % 4, 4 * w, 4)

        def xx(a_, b_):
            return v("m2", 16 * a_ + 15, 16 * b_, 16)

        def own(r):
            return v("px", 16 * r + 15, 16 * r + 16)

        def sgn(r):
            return v("sgn", 8 * r * (r - 1), 8 * r * (r + 1))
        done, z = [], (n, n)
        for x in VR[l]:
            if isinstance(x, int):
                ts(slot(x, 16 * x), bank(0, 0, 16 * x), own(x), A.is_lt)
            elif x[0] == "o":
                z = (int(x[1:]), z[0])
                tt(v("d1", *z), bank(3, z[0] - 192, z[1] - 192) if z[0] >= 192 else bank(l, *z), v("mN", 0, z[1] - z[0]), A.subtract)
            elif x == "s":
                scan(v("px", *z), v("mM", 0, z[1] - z[0]), v("d1", *z), A.min, A.max)
            elif x[0] == "A":
                r = int(x[1:])
                act(sgn(r), bank(1, 0, 16 * r), F.Sign, bias=own(r), scale=-1.0)
            elif x[0] == "B":
                r = int(x[1:])
                act(slot(r, 16 * r), sgn(r), F.Relu, accum_out=v("rr", rsum(r), rsum(r) + 1))
            elif x == "u":
                pick("sa", 0, 128, "ua", v("pl"))
                act(v("kk"), v("r16"), F.Identity, bias=cc(1))
                act(v("m2"), v("t2"), F.Identity, scale=2 * B, bias=cc(5))
            elif x == "X":
                quant("x", 192, C, v("tx", 768, 1536))
                mm(3, "sa", 0, "x", 192, C)
            elif x == "N":
                ts(v("mN"), v("t2", 0, 192), cf(1), A.not_equal, BIG, A.mult)
            elif x == "M":
                act(v("mM"), v("t2", 0, 192), F.Identity, scale=BIG, bias=-0.5 * BIG)
            elif x == "x":
                quant("x", 0, 192, v("tx", 0, 768))
                load("Y", v("tub"), T.ub[:], "dub", [v("tx")])
                dma("Y", [(ap(v("qw2"), dt.uint8), T.wc[:]), (ap(v("sw2")), T.ws[:])], "dw", [v("tx")], [v("qw2"), v("sw2")])
                load("Y", v("tv"), T.v[:], "dv", [v("tx")])
            elif x == "H":
                quant("h0", 0, 192, v("th0"))
            elif x == "n":
                quant("en", 0, 128, v("en0"))
            elif x[0] == "m":
                mm(int(x[1]), s, 0, a, 0, n)
            elif x == "g":
                quant("sg", 0, 128, v("sgB"))
            elif x[0] == "e":
                b = int(x[1])
                quant("e", 128 * b, 128 * b + 128, v("e0", 3 - b, 515 - b))
            elif x == "E":
                for b in (0, 2, 1, 3):
                    mm(4 + b, "e", 128 * b, a, 0, n)
            elif x == "d":
                tt(slot(nb, n), bank(0, 0, n), v("px", 0, n), A.is_le)
            elif x == "b":
                scan(v("rb", 0, n), v("t2", 0, n), slot(nb, n), A.min, A.add)
            elif x == "k":
                tt(xx(0, nb), v("kk", 0, nb), v("rb", 15, n, 16), A.subtract)
            elif x[0] in "wv":
                a_, b_ = (int(y) for y in x[1:].split("-"))
                tt(xx(a_, b_), xx(a_, b_), v("rr", rsum(a_), rsum(b_ - 1) + 1) if x[0] == "w" else v("rs", 192 * a_ + 191, 192 * b_, 192),
                   A.subtract)
            elif x[0] == "p":
                a_, b_ = ((0, LATE[l]), (LATE[l], n))[int(x[1])]
                part = v("iu", 24 * l + a_ // 16, 24 * l + b_ // 16)
                scan(v("sel", a_, b_), bank(3 - int(x[1]), a_, b_), v("m2", a_, b_), A.max, A.add)
                ts(part, v("sel", a_ + 15, b_, 16), 2 * B, A.add)
                copy(v("oo", oo, oo + n, ind=part), v("jj", a_, b_))
            elif x[0] == "r":
                r = int(x[1:])
                scan(v("rs", 184 * r + 192, 192 * r + 192) if r < 17 else v("rr", 0, 136), slot(r, 8 * r), slot(r, 16 * r, 8 * r), A.add, A.add)
            else:
                u = int(x[1:])
                quant("f", off[u], off[u] + wid[u], v(tiles[u]))
                if wid[u] > LATE[l]:
                    mm(2, "sg", 0, "f", off[u], off[u] + wid[u], not done, u == 1)
                mm(3, "sg", 0, "f", off[u], off[u] + min(wid[u], LATE[l]), not done, len(done) == len(tiles) - 1)
                done.append(u)
        for b in (0, 2, 1, 3):
            act(v(dd, b, 4 * n, 4), bank(4 + b, 0, n), F.Copy, scale=0.5)
        if l == 0:
            asel(v("en0"), v("e0", 0, 512), [[1, 512]], A.not_equal, -3, -4, -1.0)
            ts(v("t4"), v("t2", 0, 384, 4), cf(2), A.is_le, 5 * B, A.mult)
            quant("ub", 0, 128, v("tub"))
            quant("v", 0, 128, v("tv"))
            pick("sb", 0, 128, "ub", v("pl"))
            ts(v("m4"), v("t4"), -B, A.add)
            ts(v("nat"), v("r16", 0, 12), 0.5, A.mult, cc(8), A.add)
        else:
            pick("hn", 0, 192, "h0", v("nat"))
            post([(iu, v("lland"))], rank ^ 1, "al")
        for k in range(4):
            scan(v("sw", k * h, (k + 1) * h), v("m4", 0, h), v("oo", oo + 3 - k, oo + n, 4), A.add, A.min)
        for k in (0, 2):
            ts(v(lw, k * nb, (k + 2) * nb), v("sw", k * h + 3, (k + 2) * h, 4), 4.0, A.mult, cc(2), A.add)
        c = SPLIT[l]
        move("S", v(g3, c, n), v(dd, ind=v(lw, c // 16, nb)))
        move("V", v(g3, 0, c), v(dd, ind=v(lw, 0, c // 16)))
        move("S", v(g1, 0, n), v(dd, ind=v(lw, 2 * nb, 3 * nb)))
        tt(v("lo", 0, c) if l else v("la", 512 - c, 512), v(dd, ind=v(lw, nb, nb + c // 16)), v(g3, 0, c), A.add)
        if l == 0:
            quant("lo0", 0, 128, v("la"))
            post([(v("qlo0", 128 - c // 4, 128), v("ql0", 128, 128 + c // 4))], rank ^ 1, "a9")
        tt(v("lo", c, n) if l else v("lo", 0, n - c), v(dd, ind=v(lw, nb + c // 16, 2 * nb)), v(g3, c, n), A.add)
        tt(v("le", 512 - n, 512), v(dd, ind=v(lw, 3 * nb, 4 * nb)), v(g1), A.add)
        if l:
            quant("lo1", 0, 128, v("lo"))
            cross("lo1", 0, h, [("l1", 128, rank ^ 2)], "a1")
        else:
            quant("lo0", 128, 256, v("lo"))
            post([(v("qlo0", 128, 224 - c // 4), v("ql0", 128 + c // 4, 224)), (v("slo0", 128 - c // 4, 224 - c // 4), v("sl0", 128, 224))],
                 rank ^ 1, "a0")

    def layer(x, a, k0, h, out, qs="VVVV"):
        for b in range(4):
            mm(k0 + b, "w2", 128 * b, x, a, a + 128)
        for b in range(4):
            move(qs[b], out(b), bank(k0 + b, 128 - h, 128), 0.03125)

    down(0, "sa", "x")
    high0(0)
    quant("l0", 0, 128, v("le"))
    high0(1)
    layer("l0", 0, 0, 96, lambda b: v("ta1", b, 768, 8), "SSSS")
    layer("l0", 96, 4, 96, lambda b: v("ta1", 4 + b, 768, 8), "VSVV")
    quant("a1", 0, 192, v("ta1"))

    down(1, "sb", "a1")
    store("Y", T.ol[:], T.oo[0:128:16, :], v("oo"))
    dma("Y", [(T.lland[0:128:2, :], T.iu[0:128:2, 24:36])], "dm", [v("iu", 24, 36)], [v("lland")])
    quant("l1", 0, 128, v("le"))
    tt(v("th1", 320, 512), v("dd1", ind=v("lw1", 12, 24)), v("g31"), A.subtract)
    tt(v("th1", 128, 320), v("dd1", ind=v("lw1", 36, 48)), v("g11"), A.subtract)
    for b in range(4):
        mm(b, "w2", 128 * b, "l1", 0, 128)
    for b in range(4):
        move("SSSV"[b], v("tm", 320 + b, 512, 4), bank(b, 80, 128), 0.03125)
        if b == 0:
            quant("hh", 0, 128, v("th1"))
            cross("hh", 32, 96, [("hh", 128, rank ^ 1)], "ah")
    copy(v("yw"), v("lland"))
    quant("st", 0, 128, v("tm"))
    cross("st", 80, 48, [("st", 176, rank ^ 1)], "am")
    ts(v("yi"), v("yw"), 3, A.bitwise_and)
    layer("l1", 48, 4, 48, lambda b: v("lo", b, 192, 4))
    ts(v("yf", 0, 12), v("yi"), 2.0, A.is_ge, 188.0, A.mult)
    tt(v("yf", 12, 24), v("yi"), v("yw"), A.add)
    quant("a2", 0, 128, v("lo"))
    cross("a2", 0, 48, [("st", 128, rank ^ 2), ("st", 224, rank ^ 3)], "a2")

    def pair(w, d, b, k, a=0, e=192, c=0):
        for s, op in enumerate((A.add, A.subtract)):
            tt(v(w, 384 * b + 2 * a + s, 384 * b + 2 * e, 2), bank(k, c, c + e - a), v(d, 192 * b + a, 192 * b + e), op)

    def both(k, x, a, first):
        for s in range(2):
            mm(k + s, ("e", "en")[s if first else 0], 0 if first and s else 384, x, a, a + 192, first, not first)
    tt(v("yf", 24, 36), v("yf", 0, 12), v("yf", 12, 24), A.add)
    ts(v("c1"), v("yf", 24, 36), 0.5, A.mult, cc(6), A.add)
    for b in range(3):
        mm(b, "e", 128 * b, "hh", 32, 224)
    both(3, "hh", 32, True)
    both(5, "hn", 0, True)
    for b in range(3):
        move("S", v("dh1", 192 * b, 192 * b + 192), bank(b, 0, 192))
    mm(2, "e", 0, "hn", 0, 192)
    move("S", v("dh0", 0, 192), bank(2, 0, 192))
    for b in range(3):
        mm((7, 0, 1)[b], "e", 128 * b, "st", 0, 128)
        pair("w1", "dh1", b, (7, 0, 1)[b], 0, 48, 80)
    mm(7, "e", 0, "st", 128, 272)
    both(3, "st", 80, False)
    for b in (1, 2):
        mm(b - 1, "e", 128 * b, "st", 128, 272)
    for b in range(3):
        pair("w1", "dh1", b, (7, 0, 1)[b], 48, 192)
    for k in range(2):
        move("S", v("w1", 1152 + k, 1536, 2), bank(3 + k, 0, 192))
    for b in (1, 2):
        mm(b - 1, "e", 128 * b, "hn", 0, 192)
        move("S", v("dh0", 192 * b, 192 * b + 192), bank(b - 1, 0, 192))
    for x in UP1:
        b, a, e = int(x[1]), (0, 0, 6)[int(x[2])], (12, 6, 12)[int(x[2])]
        move(x[0], v("ta3", 64 * a + b, 64 * e, 4), v("w1", 384 * b, 384 * b + 384, ind=v("c1", a, e)))
    quant("a3", 0, 192, v("ta3"))

    mm(7, "e", 0, "a3", 0, 192)
    both(5, "a3", 0, False)
    for b in (1, 2):
        mm(b + 1, "e", 128 * b, "a3", 0, 192)
    for b in range(3):
        pair("w0", "dh0", b, (7, 2, 3)[b])
    for k in range(2):
        move("S", v("w0", 1152 + k, 1536, 2), bank(5 + k, 0, 192))
    for x in TAIL:
        u = int(x[-1])
        a, e = CUTS[u], CUTS[u + 1]
        if x[0] == "f":
            quant("fin", a, e, v("tf", 4 * a, 4 * e))
            mm(4 - 4 * u, "v", 0, "fin", a, e)
            store("Y", T.oc[:, 4 * a:4 * e], T.qfin[:, a:e].bitcast(dt.uint8), v("qfin", a, e))
            if e == C:
                dma("Y", [(T.osc[4 * k:4 * k + 4, :], T.sfin[32 * k:32 * k + 4, :]) for k in range(4)], "oh", [v("sfin")], [])
        elif x[0] == "y":
            move(x[1], v("ty", a, e), bank(4 - 4 * u, 0, e - a))
            store("S", T.y[:, a:e], T.ty[:, a:e], v("ty", a, e))
        else:
            b = int(x[1])
            move(x[0], v("tf", 4 * a + b, 4 * e, 4), v("w0", 384 * b, 384 * b + 384, ind=v("iu", a // 16, e // 16)))
    for k in ORDER or range(len(calls)):
        q, issue, reads, writes = calls[k]
        need(q, reads, writes)
        e = issue()
        note((e, cnt[e]), reads if e in Q else [], writes)
    for n in SEMAPHORES:
        if cnt[n] and seen["G"].get(n, 0) < cnt[n]:
            g.wait_ge(T.sem[n], cnt[n])
